import numpy as np, ml_dtypes
CORES = [13,21,141,149]
N = 4
BF = ml_dtypes.bfloat16
def gentries(a):
    return np.ascontiguousarray(a.reshape(8, 16, -1).transpose(0, 2, 1)).reshape(8, -1)
def gtable(e):
    e = np.asarray(e); return np.ascontiguousarray(e.reshape(8, -1, 16).transpose(0, 2, 1)).reshape(128, -1).astype(np.int32)
V, H, PP, RO, S = 2048, 8192, 256, 4, 1
TH = 6
def slot(y, w1, w2):
    u1 = np.sum(y * w1[..., None], axis=-2) & 4095; u2 = np.sum(y * w2[..., None], axis=-2) & 4095
    return (((u1 * u2) >> 5) + u2) & (H - 1)
def keys(y):
    return np.ascontiguousarray((y & 255).astype(np.uint8).T).view("S16").reshape(-1)
def index(y):
    k = keys(y); o = np.argsort(k); return k[o], o
def find(ix, q):
    ks, o = ix; kq = keys(q); pos = np.minimum(np.searchsorted(ks, kq), len(ks) - 1)
    return np.where(ks[pos] == kq, o[pos], -1)
def weights(rng):
    return rng.integers(0, 16, (N, 8, 16)), rng.integers(0, 16, (N, 8, 16))
def themes(rng):
    return rng.integers(-6, 7, (8, TH, 16)) * (rng.random((8, TH, 16)) < 0.6)
def choose(rng, w1, w2, cand, bare=False):
    c = np.concatenate([cand[:, np.all((cand >= 0) & (cand <= 127), axis=0)], rng.integers(0, 128, (16, 2 * H))], axis=1)
    h = slot(c, w1, w2)
    if bare: c, h = c[:, h > 0], h[h > 0]
    i = np.sort(np.unique(h, return_index=True)[1])[:V]
    return c[:, rng.permutation(i)]
def song(rng, w1, w2, D, top=None, first=None, alpha=None, off=None, bare=()):
    if top is None: top = np.full((8, 16, 1), 128)
    if first is None: first = np.zeros((8, 16, 0), np.int64)
    if off is None: off = np.zeros((8, 16, 1), np.int64)
    al = np.full(TH, 3.0) if alpha is None else np.asarray(alpha, float)
    y = np.zeros((N, 8, 16, V), np.int64)
    for g in range(8):
        p = np.append(0.7 * rng.dirichlet(al), 0.3); E = np.ascontiguousarray(D[g].T); M = off.shape[2]
        for k in range(N):
            r = k * S % N; img = np.zeros((16, 0), np.int64)
            if k > 0:
                s = rng.choice(TH + 1, V, p=p); m = np.flatnonzero(s < TH)
                img = y[(r - S) % N, g][:, m] + E[:, s[m]] + off[g][:, rng.integers(0, M, len(m))]
            if k == N - 1:
                s = rng.choice(TH + 1, V, p=p); m = np.flatnonzero(s < TH)
                img = np.concatenate([img, y[0, g][:, m] - E[:, s[m]] + off[g][:, rng.integers(0, M, len(m))]], axis=1)
                img = img[:, rng.permutation(img.shape[1])]
            y[r, g] = choose(rng, w1[r, g], w2[r, g], np.concatenate([first[g], img, rng.integers(0, top[g], (16, V))], axis=1), g in bare)
    return y, [[index(y[r, g]) for g in range(8)] for r in range(N)]
def hits(y, ix, r, g, d):
    b = find(ix[r][g], y[(r - S) % N, g] + d[:, None]); a = np.flatnonzero(b >= 0)
    return a, b[a]
def main(y, ix, D, g):
    return int(np.argmax([sum(len(hits(y, ix, r, g, D[g, k])[0]) for r in range(N)) for k in range(TH)]))
def pick(rng, y, ix, r, g, d, n):
    a, b = hits(y, ix, r, g, d)
    if len(a) == 0: return rng.integers(0, V, (2, n))
    i = rng.integers(0, len(a), n); return np.stack([a[i], b[i]])
def pairs(rng, y, ix, D):
    pr = np.zeros((N, 8, 2, PP), np.int64); n = PP // 16
    for r in range(N):
        for g in range(8):
            o = rng.permutation(TH)
            tail = np.concatenate([pick(rng, y, ix, r, g, D[g, k], n) for k in o[2:]] + [rng.integers(0, V, (2, 4 * n))], axis=1)
            pr[r, g] = np.concatenate([pick(rng, y, ix, r, g, D[g, o[0]], 4 * n), pick(rng, y, ix, r, g, D[g, o[1]], 4 * n), tail[:, rng.permutation(8 * n)]], axis=1)
    return pr
def race(rng, w1, w2, y, ix, g):
    E = rng.integers(-2, 3, (N, 16))
    for k in range(N):
        r = k * S % N; img = np.zeros((16, 0), np.int64)
        if k > 0:
            img = y[(r - S) % N, g][:, rng.permutation(V)] + E[r][:, None]; img = img[:, np.all((img >= 0) & (img <= 127), axis=0)]
            img = img[:, np.sort(np.unique(slot(img, w1[r, g], w2[r, g]), return_index=True)[1])[:V // 4 + int(r == N - 1)]]
        y[r, g] = choose(rng, w1[r, g], w2[r, g], img); ix[r][g] = index(y[r, g])
    return E
def pack(y, w1, w2, pr):
    return {"x": np.ascontiguousarray(y.reshape(N, 128, V)).astype(np.int32), "w1": w1.reshape(N, 128, 1).astype(np.int32), "w2": w2.reshape(N, 128, 1).astype(np.int32),
            "pa": np.stack([gtable(a[:, 0]) for a in pr]), "pb": np.stack([gtable(a[:, 1]) for a in pr])}
def setup_inputs(rng):
    w1, w2 = weights(rng); D = themes(rng); y, ix = song(rng, w1, w2, D); pr = pairs(rng, y, ix, D)
    g, h = rng.permutation(8)[:2]; m = main(y, ix, D, g)
    for r in range(N): pr[r, g] = pick(rng, y, ix, r, g, D[g, m], PP)
    q = int(rng.integers(0, N)); pr[q, h] = pick(rng, y, ix, q, h, D[h, main(y, ix, D, h)], PP)
    return pack(y, w1, w2, pr)
def setup_inputs_ties(rng):
    w1, w2 = weights(rng); D = themes(rng); y, ix = song(rng, w1, w2, D); E = race(rng, w1, w2, y, ix, 6); pr = pairs(rng, y, ix, D)
    one = np.repeat(np.array([[V - 1], [0]]), PP, axis=1)
    for g in range(8):
        m = main(y, ix, D, g)
        for r in range(N):
            if g % 4 == 0 or (g % 4 == 3 and r == 0): pr[r, g] = one
            elif g % 4 != 2: pr[r, g] = pick(rng, y, ix, r, g, D[g, m], PP)
    pr[0, 6] = rng.integers(0, V, (2, PP))
    for r in range(1, N): pr[r, 6] = pick(rng, y, ix, r, 6, E[r], PP)
    return pack(y, w1, w2, pr)
def setup_inputs_near(rng):
    w1, w2 = weights(rng); D = themes(rng); off = np.zeros((8, 16, 10), np.int64); c = np.arange(8) % 4
    for g in range(8):
        i, j, z = 2 * g, 2 * g + 1, min(2 * g, 12)
        w1[:, g, z:z + 4] = 0; w2[:, g, z:z + 4] = 0
        off[g, i, 4] = 1; off[g, j, 5] = -1; off[g, i, 6] = 1; off[g, j, 6] = -1; off[g, j, 7] = 2
        off[g, z:z + 4, 8] = np.array([1, -3, 3, -1]); off[g, z:z + 4, 9] = np.array([-1, 3, -3, 1])
    D[:, 0] = -(1 + c)[:, None]; D[4, 0] = 1
    first = np.tile(np.stack([c, 1 + c, 127 + 0 * c], axis=1)[:, None, :], (1, 16, 1))
    y, ix = song(rng, w1, w2, D, first=first, alpha=[9, 3, 3, 3, 3, 3], off=off, bare=(2, 6)); pr = pairs(rng, y, ix, D)
    for g in range(8):
        for r in range(N):
            if g % 2 == 0 or r == 0: pr[r, g, :, :PP // 2] = pick(rng, y, ix, r, g, D[g, 0], PP // 2)
    return pack(y, w1, w2, pr)
def setup_inputs_same(rng):
    w1, w2 = weights(rng); D = themes(rng); D[::2, 0] = 0; D[1, 0] = 0; D[:, 2] = -D[:, 1]
    w1[:, 1] = w1[0, 1].copy(); w2[:, 1] = w2[0, 1].copy()
    first = [rng.integers(0, 128, (16, 64)) for g in range(8)]; first[1] = choose(rng, w1[0, 1], w2[0, 1], first[1])[:, :7 * V // 8]
    y, ix = song(rng, w1, w2, D, first=first, alpha=[6, 3, 3, 3, 3, 3]); pr = pairs(rng, y, ix, D)
    for g in (0, 1, 2, 4, 6):
        for r in range(0, N, 2): pr[r, g, :, :PP // 4] = pick(rng, y, ix, r, g, D[g, 0], PP // 4)
    return pack(y, w1, w2, pr)
def setup_inputs_late(rng):
    w1, w2 = weights(rng); D = themes(rng); y, ix = song(rng, w1, w2, D); pr = np.zeros((N, 8, 2, PP), np.int64)
    for g in range(8):
        m = main(y, ix, D, g); dead = np.zeros((N, V), bool)
        for r in range(N):
            a, b = hits(y, ix, r, g, D[g, m]); dead[(r - S) % N, a] = True; dead[r, b] = True
        for r in range(N):
            c = (r - S) % N; fa = np.flatnonzero(~dead[c]); fb = np.flatnonzero(~dead[r])
            if len(fa) == 0: fa = np.array([0])
            if len(fb) == 0: fb = np.array([0])
            q = pick(rng, y, ix, r, g, D[g, m], PP - 1)
            if g % 2 == 1:
                z = rng.random(PP - 1) < 0.5; late = np.arange(PP - 1) > 0
                q = np.stack([np.where(z & late, rng.choice(fa, PP - 1), q[0]), np.where(~z & late, rng.choice(fb, PP - 1), q[1])])
            ca, cb = hits(y, ix, r, g, D[g, (m + 1 + (r + g) % (TH - 1)) % TH]); ok = ~dead[c, ca] & ~dead[r, cb]; ca, cb = ca[ok], cb[ok]
            if len(ca) == 0: ca, cb = fa[:1], fb[:1]
            j = int(rng.integers(0, len(ca)))
            pr[r, g] = np.concatenate([q, np.array([[ca[j]], [cb[j]]])], axis=1)
    return pack(y, w1, w2, pr)
def setup_inputs_spread(rng):
    ws = np.array([0, 1, 2, 7, 15]); w1 = rng.choice(ws, (N, 8, 16)); w2 = rng.choice(ws, (N, 8, 16))
    top = 2 ** rng.integers(1, 8, (8, 16, 1)); top[:, ::5] = 128
    D = rng.integers(-1, 2, (8, TH, 16)) * 2 ** rng.integers(0, 6, (8, TH, 16)) * (rng.random((8, TH, 16)) < 0.5)
    D = np.where(top.reshape(8, 1, 16) < 128, np.abs(D), D)
    e = int(rng.integers(0, 8)); top[e, 1] = 1; D[e, :, 1] = 0; D[e, 0] = 0; D[e, 0, 1] = 127; D[e, 1, 1] = -127
    y, ix = song(rng, w1, w2, D, top=top); pr = pairs(rng, y, ix, D)
    for r in range(N): pr[r, e, :, :PP // 2] = pick(rng, y, ix, r, e, D[e, 0], PP // 2)
    return pack(y, w1, w2, pr)
def check_inputs(d):
    bad = []
    for k, hi in (("x", 127), ("w1", 15), ("w2", 15), ("pa", V - 1), ("pb", V - 1)):
        if np.min(d[k]) < 0 or np.max(d[k]) > hi: bad.append("range of " + k)
    h = np.sort(slot(d["x"].astype(np.int64).reshape(N, 8, 16, V), d["w1"].astype(np.int64).reshape(N, 8, 16), d["w2"].astype(np.int64).reshape(N, 8, 16)), axis=-1)
    if np.any(h[..., 1:] == h[..., :-1]): bad.append("two notes of a rank and group have one slot number")
    return bad
def reference(x, w1, w2, pa, pb):
    y = x.astype(np.int64).reshape(N, 8, 16, V)
    la = np.stack([gentries(a) for a in pa]).astype(np.int64); lb = np.stack([gentries(a) for a in pb]).astype(np.int64)
    ix = [[index(y[r, g]) for g in range(8)] for r in range(N)]
    cov = np.zeros((N, 8, V), np.int64); win = np.zeros((8, 2 * RO), np.int64)
    for t in range(RO):
        new = cov + 0
        for g in range(8):
            best, top, won = -1, -1, []
            for d in range(N):
                c = (d - S) % N
                free = np.flatnonzero((cov[c, g][la[d, g]] == 0) & (cov[d, g][lb[d, g]] == 0))
                if len(free) == 0: continue
                k = int(free[0]); D = y[d, g][:, lb[d, g, k]] - y[c, g][:, la[d, g, k]]
                fit = []
                for r in range(N):
                    e = (r - S) % N; b = find(ix[r][g], y[e, g] + D[:, None])
                    p = np.flatnonzero((b >= 0) & (cov[e, g] == 0) & (cov[r, g][np.maximum(b, 0)] == 0))
                    fit.append((p, b[p]))
                n = sum(len(p) for p, b in fit)
                if n > top: best, top, won = d, n, fit
            win[g, t] = best; win[g, RO + t] = top
            for r in range(len(won)):
                p, b = won[r]; new[(r - S) % N, g, p] = t + 1; new[r, g, b] = t + 1
        cov = new
    return {"yc": cov.astype(np.float32), "yw": np.stack([win] * N).astype(np.float32)}

@@ -1,0 +1,619 @@
+from concourse.bass import DstId, RemoteDMATransfer
+from concourse.mybir import AluOpType, AxisListType, ActivationFunctionType
+
+V, PP, RO = 2048, 256, 4
+TW = 12288
+TD = TW + V
+BIG = 4000.0
+NOD = -300.0
+LIFT = 192.0 * 4096
+PLAN = {"a": [(0, 0, 512), (0, 1024, 512), (1, 0, 512), (1, 1024, 512), (2, 0, 512), (2, 1024, 256)],
+        "v": [(3, 0, 1024), (3, 1024, 1024), (2, 1536, 512)], "lag": 700.0}
+
+F32, BF, I32, U16 = "float32", "bfloat16", "int32", "uint16"
+SCRATCH = {}
+for _dt, _bufs in (
+    (F32, dict(tab=TD, kb=V, xf=V, pc=1536, sc=512, crow=8, zer=8, up=256, us=256, pos=128, off=128, bb=128, bt=128, qq=128, fit=512, thr=512,
+               mtmp=8, av=24, ba=4, cn=4, mk=4, ns=4, sel=16, dw=4, br=4, yt=4, kmin=4, io8=8, res=136, wf=4, jj=144, j32=128, jg=128, jy=128,
+               cf=24, idf=128, sg=128, e16=16, onef=128)),
+    (BF, dict(xb=V, xn=V, pn=V, sn=V, ab=2048, eb=2048, fc=1024, kq=512, dbc=128, mone=128, nid=128, wm4=512, k2=136, nf=128, cov=128, pf=512,
+              dall=272, dtmp=256, dm=16, msk=16, cd=4, cr=2, zf=144, zr=144, yf=144, yh=144, yr=144, zw1=144, zw2=144, kk=136, idb=128, rr=128,
+              bg=128, bgs=128, bw=256, wm=256, kr=256, oneb=128)),
+    (I32, dict(xi=V, hs=512, hm=512, ssrc=40, sm=40, smn=16, li=64, pi=4, ci=12)),
+    (U16, dict(lf=512, lr=128, kl=128, ks=8, ofw=8, l7=64, lp=32)),
+):
+    for _k, _n in _bufs.items():
+        SCRATCH[_k] = ("sbuf", [128, _n], _dt)
+SCRATCH.update({"rs": ("dram", [128, 17], I32), "rb": ("dram", [128, 256], BF), "ro": ("dram", [128, 136], F32),
+                "ds": ("dram", [8, 128, 17], I32), "db": ("dram", [8, 128, 256], BF), "df": ("dram", [4, 128, 136], F32)})
+for _k in ("m0", "m1", "m2", "m3", "st0", "st1", "ka", "pq"):
+    SCRATCH[_k] = ("psum", [128, 512], F32)
+SEMAPHORES = ["cv", "ca", "cp", "cg", "lsm", "lx0", "lx1", "lxo", "osm", "ob", "gsm", "gx0", "gx1", "gp", "gs", "of", "fin",
+              "asm", "ab0", "ab1", "af", "rsm", "rbig", "rfin", "sent"]
+
+
+def bits(engs):
+    m = 0
+    for e in engs:
+        m |= 1 << e
+    return m
+
+
+def routes(T, topo, c):
+    n = len(T.cores)
+    me = T.cores[c]
+    others = [(c + k) % n for k in range(1, n)]
+    near = [d for d in others if topo.may_write(me, T.cores[d])]
+    far = [d for d in others if d not in near]
+    mates = [k for k in topo.cores_of(me) if k not in T.cores]
+    able = [k for k in mates if all(topo.may_write(k, T.cores[d]) for d in far)]
+    same = [k for k in able if topo.die(k) == topo.die(me)]
+    rest = [k for k in able if topo.die(k) != topo.die(me)]
+    spare = [k for k in mates if k not in able and topo.die(k) != topo.die(me) and topo.may_write(k, T.cores[near[0]])]
+    off = topo.engines(me, T.cores[near[0]])
+    on = [e for e in topo.engines(me, same[0]) if e not in off]
+    q = len(on) // 2
+    p = q // 2
+    return [dict(h=0, d=far[0], via=same[0], small=on[0:p], big=on[0:q], last=on[0:q]),
+            dict(h=0, d=far[1], via=same[1], small=on[p:q], big=on[q:], last=None),
+            dict(h=0, d=near[0], via=None, small=off[0:q], big=off, last=off),
+            dict(h=1, d=far[0], via=rest[0], small=on[q:q + p], big=on[0:q], last=None),
+            dict(h=1, d=far[1], via=rest[1], small=on[q + p:], big=on[q:], last=on[q:]),
+            dict(h=1, d=near[0], via=spare[0], small=off[q:], big=off[q:], last=None)]
+
+
+def relay_program(g, core, T, topo):
+    for c in range(len(T.cores)):
+        for w in routes(T, topo, c):
+            if w["via"] != core:
+                continue
+            h, dst = w["h"], T.cores[w["d"]]
+            rid, pid = topo.addr(dst, core)
+            m = topo.mask(core, dst)
+            n = len(topo.engines(core, dst))
+            g.wait_ge(T.sem.rsm, len(w["small"]))
+            g.remote_dma(T.ds[4 * h + c], T.rs[:], T.sem.asm, T.sem.sent, pid, rid, m)
+            g.wait_ge(T.sem.rbig, len(w["big"]))
+            g.remote_dma(T.db[4 * h + c], T.rb[:], T.sem["ab%d" % h], T.sem.sent, pid, rid, m)
+            tot = 2 * n
+            if w["last"]:
+                g.wait_ge(T.sem.rfin, len(w["last"]))
+                g.remote_dma(T.df[c], T.ro[:], T.sem.af, T.sem.sent, pid, rid, m)
+                tot += n
+            g.wait_ge(T.sem.sent, tot)
+
+
+def rank_program(g, core, T, topo):
+    c = T.rank_of(core)
+    if c is None:
+        relay_program(g, core, T, topo)
+        return
+    A, F = AluOpType, ActivationFunctionType
+    Q = {"v": g.vector, "a": g.scalar, "p": g.tensor, "g": g, "s": g.sync}
+    vec, act, pe = g.vector, g.scalar, g.tensor
+
+    know = {q: {} for q in Q}
+    snap, cnt, wr, rd, seen = {}, {}, {}, {}, {}
+
+    def need(q, tok):
+        s, n = tok
+        if know[q].get(s, 0) >= n:
+            return
+        Q[q].wait_ge(T.sem[s], n)
+        seen[s] = max(seen.get(s, 0), n)
+        know[q][s] = n
+        for k, m in snap.get(tok, {}).items():
+            if know[q].get(k, 0) < m:
+                know[q][k] = m
+
+    def before(q, reads, writes):
+        toks = []
+        for t in reads:
+            if t.startswith("ps"):
+                continue
+            toks += wr.get(t, [])
+        for t in writes:
+            if not t.startswith("ps"):
+                toks += wr.get(t, []) + rd.get(t, [])
+        for t in reads + writes:
+            if t.startswith("ps"):
+                toks += [k for k in wr.get(t, []) if k[0] != "c" + q]
+        top = {}
+        for s, n in toks:
+            top[s] = max(top.get(s, 0), n)
+        for s in sorted(top, key=lambda k: k == "c" + q):
+            need(q, (s, top[s]))
+
+    def after(tok, reads, writes):
+        for t in reads:
+            if t.startswith("ps"):
+                wr[t] = [tok]
+            else:
+                rd.setdefault(t, []).append(tok)
+        for t in writes:
+            wr[t] = [tok]
+            rd[t] = []
+
+    def op(q, fn, reads, writes):
+        reads, writes = reads.split(), writes.split()
+        before(q, reads, writes)
+        s = "c" + q
+        cnt[s] = cnt.get(s, 0) + 1
+        fn().then_inc(T.sem[s], 1)
+        snap[(s, cnt[s])] = dict(know[q])
+        after((s, cnt[s]), reads, writes)
+
+    def dmas(q, s, moves, reads, writes):
+        reads, writes = reads.split(), writes.split()
+        before(q, reads, writes)
+        for o, i in moves:
+            Q[q].dma_start(o, i).then_inc(T.sem[s], 16)
+        cnt[s] = cnt.get(s, 0) + 16 * len(moves)
+        snap[(s, cnt[s])] = dict(know[q])
+        after((s, cnt[s]), reads, writes)
+
+    def arrives(s, n, tag):
+        cnt[s] = n
+        wr.setdefault(tag, []).append((s, n))
+
+    def mm(calls, reads, writes):
+        def run():
+            last = None
+            for a in calls:
+                last = pe.matmul(*a)
+            return last
+        op("p", run, reads, writes)
+
+    def ts(out, in0, s1, s2, o0, o1, reads, writes):
+        if o1 is None:
+            op("v", lambda: vec.tensor_scalar(out, in0, s1, None, o0), reads, writes)
+        else:
+            op("v", lambda: vec.tensor_scalar(out, in0, s1, s2, o0, o1), reads, writes)
+
+    def tt(out, a, b, o, reads, writes):
+        op("v", lambda: vec.tensor_tensor(out, a, b, o), reads, writes)
+
+    def cp(out, a, reads, writes):
+        op("v", lambda: vec.tensor_copy(out, a), reads, writes)
+
+    def ms(out, val, writes):
+        op("v", lambda: vec.memset(out, val), "", writes)
+
+    def ac(out, a, f, bias, scale, reads, writes):
+        op("a", lambda: act.activation(out, a, f, bias=bias, scale=scale), reads, writes)
+
+    def io(out, pat, base, mul, writes, whole=False):
+        if whole:
+            op("g", lambda: g.iota(out, pat, base, mul), "", writes)
+        else:
+            op("g", lambda: g.iota(out, pat, base, mul, allow_small_or_imprecise_dtypes=True), "", writes)
+
+    def weave(*seqs):
+        seqs = [list(s) for s in seqs]
+        while any(seqs):
+            for s in seqs:
+                if s:
+                    s.pop(0)()
+
+    ways = routes(T, topo, c)
+    sent = [0]
+
+    def send(ws, kind, src, there, on_way, sems, reads):
+        trs = []
+        for w in ws:
+            k, dst, sem = (T.cores[w["d"]], there(w), sems[0]) if w["via"] is None else (w["via"], on_way, sems[1])
+            rid, pid = topo.addr(k, core)
+            sent[0] += len(w[kind])
+            trs.append(RemoteDMATransfer(dst_ids=[DstId(rid=rid, pnc=pid)], dma_engine_mask=bits(w[kind]), remote_sem=T.sem[sem], src=src(w), dst=dst))
+        before("g", reads.split(), [])
+        g.remote_dma_fused(trs, local_sem=T.sem.sent)
+
+    def coming(kind, hs):
+        n = 0
+        for d in range(len(T.cores)):
+            if d != c:
+                for w in routes(T, topo, d):
+                    if w["d"] == c and w["h"] in hs and w[kind]:
+                        n += len(w[kind]) if w["via"] is None else len(topo.engines(w["via"], core))
+        return n
+
+    dmas("a", "lsm", [(T.ssrc[:, 0:16], T.pa[:]), (T.ssrc[:, 16:17], T.w1[:]), (T.ssrc[:, 20:36], T.pb[:]), (T.ssrc[:, 36:37], T.w2[:])], "", "ssrc")
+
+    def xload(h, d, at):
+        return (T.xi[:, at:at + 256], T.x[32 * d:32 * d + 32, 1024 * h:1024 * h + 1024])
+    dmas("s", "lx0", [xload(0, w["d"], 256 * k) for k, w in enumerate(ways[0:3])], "", "xi0")
+    dmas("a", "lx1", [xload(1, w["d"], 768 + 256 * k) for k, w in enumerate(ways[3:6])], "", "xi1")
+    dmas("a", "lxo", [xload(h, c, 1536 + 256 * h) for h in range(2)], "", "xi2")
+
+    ms(T.kb[:], BIG, "kb")
+    io(T.pi[:], [[32, 4]], 0, 1, "pi", True)
+    io(T.jj[:], [[1, 144]], -15, 0, "jj")
+    io(T.jg[:], [[16, 8], [0, 16]], 0, 0, "jg")
+    io(T.j32[:], [[0, 4], [1, 32]], 0, 0, "j32")
+    for k in (0, 1, 2, 3, 5):
+        op("a", lambda: act.activation(T.tab[:, V * k:V * k + V], T.kb[:], F.Silu), "kb", "tab%d" % k)
+
+    p = T.pi[:, 0:1]
+    ts(T.ci[:, 0:4], T.pi[:], 112, None, A.bitwise_and, None, "pi", "ci0")
+    ts(T.ci[:, 4:5], p, 15, None, A.bitwise_and, None, "pi", "ci1")
+    ts(T.ci[:, 5:6], p, 31, None, A.bitwise_and, None, "pi", "ci2")
+    ts(T.ci[:, 6:7], p, 3, 1, A.logical_shift_right, A.bitwise_and, "pi", "ci3")
+    ts(T.ci[:, 7:8], p, 1, 7, A.logical_shift_right, A.bitwise_and, "pi", "ci4")
+
+    send(ways, "small", lambda w: T.ssrc[:, 20 * w["h"]:20 * w["h"] + 17], lambda w: T.ds[4 * w["h"] + c], T.rs[:], ("asm", "rsm"), "ssrc")
+    dmas("s", "osm", [(T.ds[4 * h + c], T.ssrc[:, 20 * h:20 * h + 17]) for h in range(2)], "ssrc", "ds")
+    for h in range(2):
+        cp(T.xb[:, 768 * h:768 * h + 768], T.xi[:, 768 * h:768 * h + 768], "xi%d" % h, "xb%d" % h)
+        send(ways[3 * h:3 * h + 3], "big", lambda w: T.xb[:, 256 * ways.index(w):256 * ways.index(w) + 256], lambda w: T.db[4 * h + c], T.rb[:],
+             ("ab%d" % h, "rbig"), "xb%d" % h)
+        if h == 0:
+            ts(T.ci[:, 8:9], p, 1, None, A.bitwise_and, None, "pi", "ci5")
+            ts(T.ci[:, 9:10], p, 4, 1, A.logical_shift_right, A.bitwise_and, "pi", "ci6")
+            ts(T.ci[:, 10:11], p, 5, None, A.logical_shift_right, None, "pi", "ci7")
+            cp(T.ci[:, 11:12], p, "pi", "ci8")
+    cp(T.xb[:, 1536:2048], T.xi[:, 1536:2048], "xi2", "xb2")
+    dmas("s", "ob", [(T.db[4 * h + c], T.xb[:, 1536 + 256 * h:1792 + 256 * h]) for h in range(2)], "xb2", "db0 db1")
+    arrives("asm", coming("small", (0, 1)), "ds")
+    arrives("ab0", coming("big", (0,)), "db0")
+    arrives("ab1", coming("big", (1,)), "db1")
+
+    io(T.jy[:], [[0, 4], [1, 2], [0, 16]], 0, 0, "jy")
+    io(T.io8[:], [[16, 8]], 0, 0, "io8")
+    io(T.tab[:, 4 * V:5 * V], [[0, V]], int(BIG), 0, "tab4")
+
+    r0 = 32 * c
+    dmas("s", "gsm", [(T.sm[:, 0:17], T.ds[0:4, r0:r0 + 32, :]), (T.sm[:, 20:37], T.ds[4:8, r0:r0 + 32, :]),
+                      (T.smn[0:96, :], T.ds[1:4, r0:r0 + 32, 0:16]), (T.smn[96:128, :], T.ds[0, r0:r0 + 32, 0:16])], "ds", "sm")
+    for h in range(2):
+        dmas("s", "gx%d" % h, [(T.xn[:, 1024 * h:1024 * h + 1024], T.db[4 * h:4 * h + 4])], "db%d" % h, "xn%d" % h)
+    mv = []
+    for h in range(2):
+        mv += [(T.pn[32:128, 1024 * h:1024 * h + 1024], T.db[4 * h:4 * h + 3]), (T.pn[0:32, 1024 * h:1024 * h + 1024], T.db[4 * h + 3])]
+    dmas("s", "gp", mv, "db0 db1", "pn")
+    mv = []
+    for h in range(2):
+        mv += [(T.sn[0:96, 1024 * h:1024 * h + 1024], T.db[4 * h + 1:4 * h + 4]), (T.sn[96:128, 1024 * h:1024 * h + 1024], T.db[4 * h])]
+    dmas("s", "gs", mv, "db0 db1", "sn")
+
+    cp(T.cf[:, 0:12], T.ci[:], "ci0 ci1 ci2 ci3 ci4 ci5 ci6 ci7 ci8", "cf")
+    ms(T.msk[:, 8:16], 0.0, "msk2")
+
+    def col(k):
+        return T.cf[:, k:k + 1]
+    G0, G2, G6, C16, P31, HH, I2, ODD, YY, RK, PN = [col(k) for k in (0, 1, 3, 4, 5, 6, 7, 8, 9, 10, 11)]
+    ts(col(12), HH, 4.0, G6, A.mult, A.add, "cf", "c12")
+    ts(col(13), HH, 2.0, G2, A.mult, A.add, "cf", "c13")
+    ts(col(14), I2, G0, None, A.add, None, "cf", "c14")
+    ts(col(15), ODD, 511.0, 1.0, A.mult, A.add, "cf", "c15")
+    ts(col(16), C16, 128.0, float(TW), A.mult, A.add, "cf", "c16")
+    ts(col(17), RK, -1.0, 3.0, A.mult, A.add, "cf", "c17")
+    ts(col(18), HH, 2.0, G6, A.mult, A.add, "cf", "c18")
+    ts(col(19), I2, G2, None, A.add, None, "cf", "c19")
+    J0 = T.jj[:, 15:143]
+    ts(T.rr[:], T.j32[:], P31, None, A.is_equal, None, "cf j32", "rr")
+    ts(T.zf[:], T.jj[:], G6, None, A.is_equal, None, "cf jj", "zf")
+    ts(T.zr[:], T.jj[:], G2, 16384.0, A.is_equal, A.mult, "cf jj", "zr")
+    ts(T.idb[:], J0, PN, None, A.is_equal, None, "cf jj", "idb")
+    ts(T.idf[:], J0, PN, None, A.is_equal, None, "cf jj", "idf")
+    ts(T.bg[:], T.jg[:], G0, -512.0, A.is_equal, A.mult, "cf jg", "bg")
+    ts(T.bgs[:], T.jg[:], G2, -512.0, A.is_equal, A.mult, "cf jg", "bgs")
+    ts(T.yf[:], T.jj[:], col(12), None, A.is_equal, None, "c12 jj", "yf")
+    ts(T.yh[:], T.jj[:], col(18), None, A.is_equal, None, "c18 jj", "yh")
+    ts(T.yr[:], T.jj[:], col(13), 16384.0, A.is_equal, A.mult, "c13 jj", "yr")
+    ts(T.kk[:], T.jj[:, 7:143], col(14), col(15), A.is_equal, A.mult, "c14 c15 jj", "kk")
+    ts(T.k2[:], T.jj[:, 7:143], col(19), col(15), A.is_equal, A.mult, "c19 c15 jj", "k2")
+    ts(T.nid[:], J0, PN, -4096.0, A.is_equal, A.mult, "cf jj", "nid")
+    ms(T.mone[:], -1.0, "mone")
+    ms(T.crow[0:1, 0:4], -2047.5, "crow0")
+    ms(T.crow[0:1, 4:7], 0.0, "crow1")
+    ms(T.crow[0:1, 7:8], 2047.5, "crow2")
+    ts(T.off[:], J0, col(16), None, A.add, None, "c16 jj", "off")
+    ts(T.e16[:], T.jj[:, 15:31], C16, 1.0e9, A.not_equal, A.mult, "cf jj", "e16")
+    ts(T.msk[:, 0:4], T.jj[:, 15:19], RK, None, A.is_equal, None, "cf jj", "msk0")
+    ts(T.mtmp[:, 0:5], T.jj[:, 15:20], col(17), None, A.is_equal, None, "c17 jj", "mtmp")
+    ms(T.kr[0:2, :], 1024.0, "kr")
+    ts(T.e16[:], T.e16[:], float(TW), None, A.add, None, "e16", "e16")
+    tt(T.msk[:, 4:8], T.mtmp[:, 0:4], T.mtmp[:, 1:5], A.subtract, "mtmp", "msk1")
+    ms(T.dw[:, 0:3], 128.0, "dw0")
+    ms(T.dw[:, 3:4], 0.0, "dw1")
+    ms(T.ks[:], 0, "ks")
+    ms(T.zer[:], 0.0, "zer")
+    ms(T.dall[:, 256:272], NOD, "dall1")
+    ms(T.oneb[0:2, :], 1.0, "oneb")
+    ms(T.onef[0:1, :], 1.0, "onef")
+    ms(T.qq[:], 4.0, "qq")
+    ts(T.sg[:], T.jy[:], YY, 4.0, A.is_equal, A.mult, "cf jy", "sg")
+    ts(T.io8[:], T.io8[:], C16, None, A.add, None, "cf io8", "io8")
+    io(T.kr[0:1, :], [[1, 256]], 0, 0, "kr")
+    io(T.tab[:, 6 * V:7 * V], [[0, V]], int(BIG), 0, "tab6")
+
+    cp(T.wf[:, 0:2], T.sm[:, 16:37:20], "sm", "wf")
+    ts(T.li[:, 0:16], T.sm[:, 20:36], 127, None, A.bitwise_and, None, "sm", "li0")
+    for u, z in enumerate((T.zw1, T.zw2)):
+        ts(z[:], T.jj[:], G0, T.wf[:, u:u + 1], A.is_equal, A.mult, "cf jj wf", "zw%d" % u)
+    for u in range(2):
+        ts(T.bw[:, 128 * u:128 * u + 128], T.jg[:], G0, T.wf[:, u:u + 1], A.is_equal, A.mult, "cf jg wf", "bw%d" % u)
+    mm([(T.ka[:, 0:256], T.rr[:], T.bw[:], True, True)], "rr bw0 bw1", "pska")
+    ts(T.li[:, 16:32], T.smn[:], 127, None, A.bitwise_and, None, "sm", "li1")
+    ts(T.li[:, 32:48], T.sm[:, 20:36], 7, None, A.logical_shift_right, None, "sm", "li2")
+    ts(T.li[:, 48:64], T.smn[:], 7, None, A.logical_shift_right, None, "sm", "li3")
+    cp(T.lp[:, 0:16], T.sm[:, 0:16], "sm", "lp0")
+    cp(T.lp[:, 16:32], T.sm[:, 20:36], "sm", "lp1")
+    cp(T.l7[:], T.li[:], "li0 li1 li2 li3", "l7")
+    ac(T.wm[:], T.ka[:, 0:256], F.Identity, 0.0, 1.0, "pska", "wm")
+    ac(T.thr[:], T.e16[:, 0:16].indirect(T.l7[:, 32:64]), F.Identity, 0.0, 1.0, "e16 l7", "thr")
+    for d in range(4):
+        ts(T.wm4[:, 128 * d:128 * d + 128], T.wm[:, 128:256], T.msk[:, d:d + 1], None, A.mult, None, "wm msk0", "wm4%d" % d)
+
+    def places(k, n, u2, held, last, tags, out_tag):
+        a = 256 * k
+        u1, m = T.hs[:, a:a + n], T.hm[:, a:a + n]
+        hs, hm = "hs_%d" % k, "hm_%d" % k
+        return [lambda: ts(u1, u1, 4095, None, A.bitwise_and, None, tags, hs),
+                lambda: tt(m, u1, u2, A.mult, hs + " " + held, hm),
+                lambda: ts(m, m, 5, 8191, A.logical_shift_right, A.bitwise_and, hm, hm),
+                lambda: tt(m, m, u2, A.add, hm + " " + held, hm),
+                lambda: cp(last, m, hm, out_tag)]
+
+    ZW = (T.zw1, T.zw2)
+    MB = (T.m0, T.m1, T.m2, T.m3)
+    ST = (T.st0, T.st1)
+
+    def lay(k):
+        o, i = T.xf[:, k::16], T.xn[:, 128 * k:128 * k + 128]
+        if k % 2 == 0 and k < 12:
+            ts(o, i, 128.0, None, A.add, None, "xn%d" % (k // 8), "xf%d" % k)
+        else:
+            ac(o, i, F.Identity, 128.0, 1.0, "xn%d" % (k // 8), "xf%d" % k)
+    for h in range(2):
+        for u in range(2):
+            mm([(MB[u][:, 0:128], ZW[u][:, 15 - k:143 - k], T.xn[:, 128 * k:128 * k + 128], k == 0, k == 15) for k in range(8 * h, 8 * h + 8)],
+               "zw%d xn%d" % (u, h), "psm%d" % u)
+        for k in range(8 * h, 8 * h + 8):
+            lay(k)
+
+    def pack(bank, src, at, w, to=0, kk=T.kk):
+        return [(bank[:, to:to + w], kk[:, 8:136], src[:, at:at + w], True, False),
+                (bank[:, to:to + w], kk[:, 0:128], src[:, at + w:at + 2 * w], False, True)]
+    shapes = sorted(set((a, w) for d, a, w in PLAN["a"]), key=lambda s: (-s[1], s[0]))
+    pc_at, at = {}, 0
+    banks = ((T.st0, "psst0"), (T.st1, "psst1"), (T.pq, "pspq"), (T.m3, "psm3"))
+    for k, (a, w) in enumerate(shapes):
+        pc_at[a, w] = at
+        at += w
+        mm(pack(banks[k][0], T.xn, a, w, 0, T.k2), "k2 xn0 xn1", banks[k][1])
+    for k, (a, w) in enumerate(shapes):
+        ac(T.pc[:, pc_at[a, w]:pc_at[a, w] + w], banks[k][0][:, 0:w], F.Identity, 64.0 * 513, 1.0, banks[k][1], "pc%d_%d" % (a, w))
+    for u in range(2):
+        cp(T.hs[:, 128 * u:128 * u + 128], MB[u][:, 0:128], "psm%d" % u, "hs%d" % u)
+    for u in range(2):
+        mm([(MB[2 + u][:, 0:128], ZW[u][:, 15 - k:143 - k], T.pn[:, k::16], k == 0, k == 15) for k in range(16)], "zw%d pn" % u, "psm%d" % (2 + u))
+    ts(T.hs[:, 0:256], T.hs[:, 0:256], 4095, None, A.bitwise_and, None, "hs0 hs1", "hs_0")
+    tt(T.hm[:, 0:128], T.hs[:, 0:128], T.hs[:, 128:256], A.mult, "hs_0", "hm_0")
+    ts(T.hm[:, 0:128], T.hm[:, 0:128], 5, 8191, A.logical_shift_right, A.bitwise_and, "hm_0", "hm_0")
+    tt(T.pos[:], T.hm[:, 0:128], T.hs[:, 128:256], A.add, "hm_0 hs_0", "pos")
+    cp(T.kl[:], T.pos[:], "pos", "kl")
+    op("a", lambda: act.activation(T.tab[:, 0:TW].indirect(T.kl[:]), T.xf[:], F.Silu),
+       "kl " + " ".join("xf%d" % k for k in range(16)), "tab " + " ".join("tab%d" % k for k in range(6)))
+    cp(T.dtmp[:], T.pn[:, 0:V].indirect(T.lp[:, 0:16]), "pn lp0", "dtmp")
+    tt(T.dall[:, 0:256], T.xn[:, 0:V].indirect(T.lp[:, 16:32]), T.dtmp[:], A.subtract, "xn0 xn1 lp1 dtmp", "dall0")
+
+    tabw = T.tab[:, 0:TW]
+    UB, ub = T.st1, "psst1"
+
+    def u2_start():
+        mm([(UB[:, 128 * d:128 * d + 128], T.idf[:], T.up[:, 128:256], d == 0, False) for d in range(4)], "idf up1", ub)
+
+    for t in range(RO):
+        mm([(T.ka[:, 16:24], T.onef[0:1, :], T.crow[0:1, :], True, False)], "onef crow0 crow1 crow2", "pska")
+        if t == 0:
+            cp(T.up[:, 0:128], T.m2[:, 0:128], "psm2", "up0")
+            ts(T.up[:, 128:256], T.m3[:, 0:128], LIFT, None, A.add, None, "psm3", "up1")
+        tt(T.dm[:], T.dall[:, 0:272].indirect(T.ks[:, 0:1]), T.msk[:], A.mult, "dall0 dall1 ks msk0 msk1 msk2", "dm")
+        mm([(T.ka[:, 16:24], T.wm[:, 128:256], T.dm[:, 0:8], False, True), (T.ka[:, 8:16], T.wm[:, 0:128], T.dm[:, 0:8], True, True),
+            (T.ka[:, 0:8], T.rr[:], T.dm[:, 0:8], True, True)], "wm rr dm", "pska")
+        if t == 0:
+            u2_start()
+        cp(T.dbc[:], T.dall[:, 0:272].indirect(T.ks[:]), "dall0 dall1 ks", "dbc")
+        mm([(UB[:, 128 * d:128 * d + 128], T.wm4[:, 128 * d:128 * d + 128], T.dbc[:], False, False) for d in range(4)], "wm40 wm41 wm42 wm43 dbc", ub)
+        fill = []
+        cp(T.av[:], T.ka[:, 0:24], "pska", "av")
+        for d in range(4):
+            ts(T.kq[:, 128 * d:128 * d + 128], T.up[:, 128:256], T.av[:, 16 + d:17 + d], 1.0 / 4096, A.add, A.mult, "up1 av", "kq%d" % d)
+        mm([(UB[:], T.nid[:], T.kq[:], False, True)], "nid kq0 kq1 kq2 kq3", ub)
+        if t == 0:
+            for u in range(2):
+                mm([(MB[u][:, 0:128], ZW[u][:, 15 - k:143 - k], T.sn[:, k::16], k == 0, k == 15) for k in range(16)], "zw%d sn" % u, "psm%d" % u)
+                fill.append(lambda u=u: ts(T.us[:, 128 * u:128 * u + 128], MB[u][:, 0:128], LIFT * u, None, A.add, None, "psm%d" % u, "us%d" % u))
+        mm([(T.ka[:, 32:36], T.onef[0:1, :], T.jj[0:1, 15:19], True, False)], "onef jj", "pska")
+
+        def sums(k):
+            return [lambda d=d: ts(T.hs[:, 128 * d:128 * d + 128], T.up[:, 0:128], T.av[:, 8 + d:9 + d], None, A.add, None, "up0 av hs_%d" % k, "hs%d" % d)
+                    for d in (2 * k, 2 * k + 1)]
+        weave(sums(0))
+        if t > 0:
+            ts(T.cov[:], T.off[:], float(TW), None, A.is_lt, None, "off", "cov")
+            for d in range(4):
+                mm([(MB[d][:, 0:128], T.idb[:], T.cov[:], True, False)], "idb cov", "psm%d" % d)
+        weave(places(0, 256, UB[:, 0:256], ub, T.lf[:, 0:256], "hs0 hs1", "lf0"),
+              [lambda: ts(T.ba[:], T.av[:, 0:4], -1.0, -64.0, A.mult, A.add, "av", "ba")] + sums(1))
+        weave(places(1, 256, UB[:, 256:512], ub, T.lf[:, 256:512], "hs2 hs3", "lf1"),
+              [lambda: ts(T.cd[:], T.av[:, 0:4], 128.0, None, A.add, None, "av", "cd")] + fill)
+
+        begun = [t > 0] * 4
+        left = [V] * 4
+
+        def lst(d, a, n):
+            return T.lf[:, 128 * d + a // 16:128 * d + (a + n) // 16]
+
+        def into(d, z, src, at, first, n, notes, tags):
+            calls = []
+            left[d] -= notes
+            for b in range(n):
+                calls.append((MB[d][:, 0:128], z[:, 15 - first - b:143 - first - b], src[:, at + 128 * b:at + 128 * b + 128],
+                              not begun[d], left[d] == 0 and b == n - 1))
+                begun[d] = True
+            mm(calls, tags, "psm%d" % d)
+
+        def a_get(k, d, a, w):
+            ac(T.ab[:, 1024 * (k % 2):1024 * (k % 2) + 2 * w], tabw.indirect(lst(d, a, 2 * w)), F.Identity, T.ba[:, d:d + 1], 1.0,
+               "tab ba lf%d" % (d // 2), "ab%d" % (k % 2))
+
+        def a_pack(k, w):
+            mm(pack(ST[k % 2], T.ab, 1024 * (k % 2), w), "kk ab%d" % (k % 2), "psst%d" % (k % 2))
+
+        def a_cmp(k, d, a, w):
+            tt(T.fc[:, 512 * (k % 2):512 * (k % 2) + w], ST[k % 2][:, 0:w], T.pc[:, pc_at[a, w]:pc_at[a, w] + w], A.not_equal,
+               "psst%d pc%d_%d" % (k % 2, a, w), "fc%d" % (k % 2))
+
+        def a_sum(k, d, a, w):
+            into(d, T.yf if w == 512 else T.yh, T.fc, 512 * (k % 2), a // 128, w // 128, 2 * w, "yf yh fc%d" % (k % 2))
+
+        def v_get(k, d, a, n):
+            tt(T.eb[:, 1024 * (k % 2):1024 * (k % 2) + n], tabw.indirect(lst(d, a, n)), T.pn[:, a:a + n], A.subtract,
+               "tab pn lf%d" % (d // 2), "eb%d" % (k % 2))
+
+        def v_cmp(k, d, a, n):
+            e = T.eb[:, 1024 * (k % 2):1024 * (k % 2) + n]
+            ts(e, e, T.cd[:, d:d + 1], None, A.not_equal, None, "cd eb%d" % (k % 2), "eb%d" % (k % 2))
+
+        def v_sum(k, d, a, n):
+            into(d, T.zf, T.eb, 1024 * (k % 2), a // 128, n // 128, n, "zf eb%d" % (k % 2))
+
+        def count(d):
+            op("a", lambda: act.activation(T.fit[:, 128 * d:128 * d + 128], MB[d][:, 0:128], F.Relu, bias=1.0, scale=-1.0,
+                                           accum_out=T.cn[:, 3 - d:4 - d]), "psm%d" % d, "fit%d cn%d" % (d, d))
+
+        ev, full = [], [0.0] * 4
+        own = []
+        for k, u in enumerate(PLAN["v"]):
+            own += [(u[2] * 1.56 + 60, v_get, k, u), (u[2] * 0.52 + 60, v_cmp, k, u)]
+        got, packed, cmpd = [], [], []
+        tv, j = PLAN["lag"], 0
+        while j < len(PLAN["a"]) or own:
+            if j < len(PLAN["a"]) and len(packed) == j:
+                while len(got) <= j:
+                    i = len(got)
+                    s0 = max(got[-1] if got else 0.0, packed[i - 2] if i >= 2 else 0.0)
+                    ev.append((s0, len(ev), a_get, (i,) + PLAN["a"][i]))
+                    got.append(s0 + PLAN["a"][i][2] * 3.12 + 60)
+                s0 = max(got[j], cmpd[j - 2] if j >= 2 else 0.0)
+                ev.append((s0, len(ev), a_pack, (j, PLAN["a"][j][2])))
+                packed.append(s0 + PLAN["a"][j][2] * 1.04 + 160)
+            if j < len(PLAN["a"]) and (packed[j] <= tv + 150 or not own):
+                d, a, w = PLAN["a"][j]
+                tv = max(tv, packed[j])
+                ev.append((tv, len(ev), a_cmp, (j, d, a, w)))
+                tv += w * 1.04 + 60
+                cmpd.append(tv)
+                ev.append((tv, len(ev), a_sum, (j, d, a, w)))
+                full[d] = max(full[d], tv + w * 0.52 + 80)
+                j += 1
+            else:
+                dur, fn, k, u = own.pop(0)
+                ev.append((tv, len(ev), fn, (k,) + u))
+                tv += dur
+                if fn is v_cmp:
+                    ev.append((tv, len(ev), v_sum, (k,) + u))
+                    full[u[0]] = max(full[u[0]], tv + u[2] * 0.52 + 80)
+        for d in range(4):
+            ev.append((full[d], len(ev), count, (d,)))
+        for e in sorted(ev, key=lambda e: e[0:2]):
+            e[2](*e[3])
+
+        if t > 0:
+            tt(T.qq[:], T.qq[:], T.cov[:], A.subtract, "qq cov", "qq")
+        mm([(T.ka[:, 32:36], T.sg[:], T.cn[:], False, True)], "sg cn0 cn1 cn2 cn3", "pska")
+        mm([(T.pq[:, 0:128], T.idf[:], T.us[:, 128:256], True, False)], "idf us1", "pspq")
+        if t == 0:
+            mm(pack(ST[0], T.sn, 0, 256) + pack(ST[0], T.sn, 512, 256, 256), "kk sn", "psst0")
+        m = T.mk[:, t:t + 1]
+        op("v", lambda: vec.tensor_reduce(m, T.ka[:, 32:36], AxisListType.X, A.max), "pska", "mk")
+        ts(T.ns[:], T.ka[:, 32:36], m, None, A.not_equal, None, "pska mk", "ns")
+
+        def pick(k, src):
+            op("v", lambda: vec.tensor_tensor_scan(T.sel[:, 4 * k:4 * k + 4], T.ns[:], src, 0.0, A.mult, A.add), "ns av dw0 dw1", "sel%d" % k)
+        pick(2, T.av[:, 4:8])
+        pick(1, T.av[:, 20:24])
+        pick(0, T.av[:, 12:16])
+        W, w128 = T.sel[:, 11:12], T.sel[:, 15:16]
+        ac(T.dbc[:], T.mone[:], F.Identity, 0.0, W, "mone sel2", "dbc")
+        mm([(T.pq[:, 0:128], T.bw[:, 128:256], T.dbc[:], False, False)], "bw1 dbc", "pspq")
+        ts(T.kq[:, 0:128], T.us[:, 128:256], T.sel[:, 7:8], 1.0 / 4096, A.subtract, A.mult, "us1 sel1", "kq0")
+        mm([(T.pq[:, 0:128], T.nid[:], T.kq[:, 0:128], False, True)], "nid kq0", "pspq")
+        for d in range(2):
+            mm([(MB[d][:, 0:128], T.idf[:], T.pos[:], True, False)], "idf pos", "psm%d" % d)
+        ts(T.hs[:, 0:128], T.us[:, 0:128], T.sel[:, 3:4], None, A.subtract, None, "us0 sel0 hs_0", "hs0")
+        pick(3, T.dw[:])
+        weave(places(0, 128, T.pq[:, 0:128], "pspq", T.lr[:], "hs0", "lr"),
+              [lambda: ts(T.ofw[:], T.io8[:], T.sel[:, 15:16], None, A.add, None, "io8 sel3", "ofw")])
+        ac(T.br[:, 0:1], W, F.Identity, -64.0, 1.0, "sel2", "br")
+        ac(T.br[:, 1:2], W, F.Identity, -128.0, 1.0, "sel2", "br1")
+        ac(T.cr[:, 0:1], W, F.Identity, 128.0, -1.0, "sel2", "cr")
+        if t == 0:
+            ac(T.sc[:], ST[0][:], F.Identity, 64.0 * 513, 1.0, "psst0", "sc0 sc1")
+        ac(T.nf[:], T.fit[:, 0:512].indirect(T.ofw[:]), F.Identity, 16384.0, -16384.0, "fit0 fit1 fit2 fit3 ofw", "nf")
+        mm([(T.m1[:, 0:128], T.idb[:], T.nf[:], False, True)], "idb nf", "psm1")
+        ac(T.yt[:, 0:1], w128, F.Identity, 0.25, 1.0 / 512, "sel3", "yt0")
+        ac(T.yt[:, 1:2], w128, F.Identity, 1.0, 1.0 / 128, "sel3", "yt1")
+
+        def r_get(k):
+            ac(T.ab[:, 512 * k:512 * k + 512], tabw.indirect(T.lr[:, 32 * k:32 * k + 32]), F.Identity, T.br[:, 0:1], 1.0,
+               "tab lr br", "ar0 ab0" if k == 0 else "ar1")
+
+        def r_pack(k):
+            mm(pack(ST[k], T.ab, 512 * k, 256), "kk ar%d ab0" % k, "psst%d" % k)
+
+        def r_cmp(k):
+            tt(T.fc[:, 512 * k:512 * k + 256], ST[k][:, 0:256], T.sc[:, 256 * k:256 * k + 256], A.not_equal, "psst%d sc%d" % (k, k), "fc%d" % k)
+
+        def r_sum(k):
+            mm([(T.m0[:, 0:128], T.yr[:, 15 - 4 * k - b:143 - 4 * k - b], T.fc[:, 512 * k + 128 * b:512 * k + 128 * b + 128], False, k == 1 and b == 1)
+                for b in range(2)], "yr fc%d" % k, "psm0")
+
+        def z_sum(k):
+            mm([(T.m0[:, 0:128], T.zr[:, 7 - 4 * k - b:135 - 4 * k - b], T.eb[:, 1024 * k + 128 * b:1024 * k + 128 * b + 128], False, False)
+                for b in range(4)], "zr eb%d" % k, "psm0")
+        e0, e1 = T.eb[:, 0:512], T.eb[:, 1024:1536]
+        r_get(0)
+        tt(e0, tabw.indirect(T.lr[:, 64:96]), T.sn[:, 1024:1536], A.subtract, "tab lr sn", "eb0")
+        r_pack(0)
+        r_get(1)
+        tt(e1, tabw.indirect(T.lr[:, 96:128]), T.sn[:, 1536:2048], A.subtract, "tab lr sn", "eb1")
+        r_pack(1)
+        ac(e0, e0, F.Abs, T.br[:, 1:2], 1.0, "br1 eb0", "eb0")
+        r_cmp(0)
+        r_sum(0)
+        ts(e1, e1, T.cr[:, 0:1], None, A.not_equal, None, "cr eb1", "eb1")
+        z_sum(0)
+        r_cmp(1)
+        z_sum(1)
+        tt(T.bb[:], T.m1[:, 0:128], T.off[:], A.min, "psm1 off", "bb")
+        r_sum(1)
+        ac(T.yt[:, 2:3], m, F.Identity, T.yt[:, 0:1], 0.25, "mk yt0", "yt2")
+        ac(T.yt[:, 3:4], T.yt[:, 2:3], F.Sign, -1.0, 1.0, "yt2", "yt3")
+        ac(T.res[:, 128 + t:129 + t], T.yt[:, 3:4], F.Identity, -1.0, T.yt[:, 1:2], "yt3 yt1", "rw%d" % t)
+        ac(T.res[:, 132 + t:133 + t], T.yt[:, 3:4], F.Identity, -1.0, T.yt[:, 2:3], "yt3 yt2", "rc%d" % t)
+        tt(T.off[:], T.m0[:, 0:128], T.bb[:], A.min, "psm0 bb", "off")
+        if t < RO - 1:
+            cp(T.kl[:], T.off[:], "off", "kl")
+            u2_start()
+            op("a", lambda: act.activation(T.tab[:, 0:TD].indirect(T.kl[:]), T.kb[:], F.Silu), "kl kb", "tab tab6")
+            mm([(T.pq[:, 0:256], T.oneb[0:2, :], T.kr[0:2, :], True, False)], "oneb kr", "pspq")
+            tt(T.pf[:], T.off[:, 0:128].indirect(T.l7[:, 0:32]), T.thr[:], A.is_ge, "off l7 thr", "pf")
+            mm([(T.pq[:, 0:256], T.bg[:], T.pf[:, 0:256], False, False), (T.pq[:, 0:256], T.bgs[:], T.pf[:, 256:512], False, True)],
+               "bg bgs pf", "pspq")
+            op("v", lambda: vec.tensor_reduce(T.kmin[:, 0:1], T.pq[:, 0:256], AxisListType.X, A.min), "pspq", "kmin")
+            ts(T.ks[:], T.zer[:], T.kmin[:, 0:1], float(PP), A.add, A.min, "kmin zer", "ks")
+
+    ts(T.bt[:], T.off[:], float(TW), None, A.is_lt, None, "off", "bt")
+    tt(T.res[:, 0:128], T.bt[:], T.qq[:], A.mult, "bt qq", "res")
+    tags = "res " + " ".join("rw%d rc%d" % (t, t) for t in range(RO))
+    send([w for w in ways if w["last"]], "last", lambda w: T.res[:], lambda w: T.df[c], T.ro[:], ("af", "rfin"), tags)
+    dmas("s", "of", [(T.df[c], T.res[:])], tags, "df")
+    arrives("af", coming("last", (0, 1)), "df")
+    dmas("s", "fin", [(T.yc[:], T.df[:, r0:r0 + 32, 0:128]), (T.yw[:], T.df[:, 0:32:16, 128:136])], "df", "")
+    cnt["sent"] = sent[0]
+    for s in cnt:
+        if seen.get(s, 0) < cnt[s]:
+            need("g", (s, cnt[s]))

@@ -7,29 +7,34 @@ TD = TW + V
 BIG = 4000.0
 NOD = -300.0
 LIFT = 192.0 * 4096
-PLAN = {"a": [(0, 0, 512), (0, 1024, 512), (1, 0, 512), (1, 1024, 512), (2, 0, 512), (2, 1024, 256)],
-        "v": [(3, 0, 1024), (3, 1024, 1024), (2, 1536, 512)], "lag": 700.0}
+PLAN = {"a": [(0, 0, 512), (0, 1024, 512), (1, 0, 512), (1, 1024, 512), (2, 0, 384), (2, 384, 128)],
+        "v": [(3, 0, 1024), (3, 1024, 512), (3, 1536, 512), (2, 1024, 512), (2, 1536, 512)],
+        "bank": [0, 1, 0, 1, 2, 0],
+        "aq": "g0 g1 g2 g3 g4 g5 e4 n0 n3 n1 n2", "vq": "g0 c0 g1 p0 c1 g2 p1 c2 g3 p2 c3 g4 p3 c4 p5", "lag": 200.0, "ahead": 0.0}
 
 F32, BF, I32, U16 = "float32", "bfloat16", "int32", "uint16"
 SCRATCH = {}
 for _dt, _bufs in (
-    (F32, dict(tab=TD, kb=V, xf=V, pc=1536, sc=512, crow=8, zer=8, up=256, us=256, pos=128, off=128, bb=128, bt=128, qq=128, fit=512, thr=512,
-               mtmp=8, av=24, ba=4, cn=4, mk=4, ns=4, sel=16, dw=4, br=4, yt=4, kmin=4, io8=8, res=136, wf=4, jj=144, j32=128, jg=128, jy=128,
-               cf=24, idf=128, sg=128, e16=16, onef=128)),
-    (BF, dict(xb=V, xn=V, pn=V, sn=V, ab=2048, eb=2048, fc=1024, kq=512, dbc=128, mone=128, nid=128, wm4=512, k2=136, nf=128, cov=128, pf=512,
-              dall=272, dtmp=256, dm=16, msk=16, cd=4, cr=2, zf=144, zr=144, yf=144, yh=144, yr=144, zw1=144, zw2=144, kk=136, idb=128, rr=128,
-              bg=128, bgs=128, bw=256, wm=256, kr=256, oneb=128)),
-    (I32, dict(xi=V, hs=512, hm=512, ssrc=40, sm=40, smn=16, li=64, pi=4, ci=12)),
+    (F32, dict(tab=TD, kb=1024, xf=V, pc=1536, crow=8, zer=8, up=256, us=256, pos=128, off=128, bb=128, fit=512, thr=512,
+               mtmp=8, av=24, ba=4, cn=4, mk=4, ns=4, sel=12, sw=16, dw=4, br=4, yt=16, kmin=4, io8=8, res=128, ryw=8, wf=8, jj=144, jw=164,
+               j32=128, jg=128, jy=128, cf=28, idf=128, sg=128, e16=16, onef=128)),
+    (BF, dict(xb=V, xn=V, pn=V, sn=V, ab=3072, eb=3072, fc=1536, kq=512, dbc=128, mone=128, nid=128, wm4=512, k2=136, nk2=136, nf=128, cov=512, pf=512,
+              dall=272, dtmp=512, dm=16, msk=16, cd=4, cr=2, zf=144, zr=144, yf=144, yh=144, yr=144, zw0=144, zw1=144, zn0=144, zn1=144,
+              zp0=144, zp1=144, kk=136, nkk=136, idb=128, rr=128, bg=128, bgs=128, bw=256, wm=256, kr=256, oneb=128, shn=128, nshp=128,
+              wfb=2, rl=4 * 164)),
+    (I32, dict(xi=V, hs=512, hm=512, ph=192, sm=32, wi=8, li=96, pi=4, ci=16)),
     (U16, dict(lf=512, lr=128, kl=128, ks=8, ofw=8, l7=64, lp=32)),
 ):
     for _k, _n in _bufs.items():
         SCRATCH[_k] = ("sbuf", [128, _n], _dt)
-SCRATCH.update({"rs": ("dram", [128, 17], I32), "rb": ("dram", [128, 256], BF), "ro": ("dram", [128, 136], F32),
-                "ds": ("dram", [8, 128, 17], I32), "db": ("dram", [8, 128, 256], BF), "df": ("dram", [4, 128, 136], F32)})
+SCRATCH.update({"st": ("dram", [4, 136, 8], I32), "rs": ("dram", [128, 8], I32), "ds": ("dram", [8, 128, 8], I32),
+                "rb": ("dram", [128, 256], BF), "db": ("dram", [8, 128, 256], BF),
+                "rw": ("dram", [128, 2], F32), "dy": ("dram", [4, 128, 2], F32),
+                "ro": ("dram", [128, 32], F32), "df": ("dram", [4, 128, 32], F32)})
 for _k in ("m0", "m1", "m2", "m3", "st0", "st1", "ka", "pq"):
     SCRATCH[_k] = ("psum", [128, 512], F32)
-SEMAPHORES = ["cv", "ca", "cp", "cg", "lsm", "lx0", "lx1", "lxo", "osm", "ob", "gsm", "gx0", "gx1", "gp", "gs", "of", "fin",
-              "asm", "ab0", "ab1", "af", "rsm", "rbig", "rfin", "sent"]
+SEMAPHORES = ["cv", "ca", "cp", "cg", "lw", "ow", "as0", "as1", "lsm", "lx0", "lx1", "lx2", "lx3", "lx4", "lx5", "osm", "ob0", "ob1", "gw", "gsm", "gx0", "gx1", "gy0", "gy1",
+              "gp", "gs", "of", "oy", "fin", "fiy", "an0", "an1", "af0", "af1", "ay", "al", "rsm", "rbig", "rwin", "rlast", "sent"]
 
 
 def bits(engs):
@@ -45,21 +50,20 @@ def routes(T, topo, c):
     others = [(c + k) % n for k in range(1, n)]
     near = [d for d in others if topo.may_write(me, T.cores[d])]
     far = [d for d in others if d not in near]
-    mates = [k for k in topo.cores_of(me) if k not in T.cores]
-    able = [k for k in mates if all(topo.may_write(k, T.cores[d]) for d in far)]
+    chip = [k for k in topo.cores_of(me) if k not in T.cores]
+    able = [k for k in chip if all(topo.may_write(k, T.cores[d]) for d in far)]
     same = [k for k in able if topo.die(k) == topo.die(me)]
     rest = [k for k in able if topo.die(k) != topo.die(me)]
-    spare = [k for k in mates if k not in able and topo.die(k) != topo.die(me) and topo.may_write(k, T.cores[near[0]])]
+    spare = [k for k in chip if k not in able and topo.die(k) != topo.die(me) and topo.may_write(k, T.cores[near[0]])]
     off = topo.engines(me, T.cores[near[0]])
     on = [e for e in topo.engines(me, same[0]) if e not in off]
     q = len(on) // 2
-    p = q // 2
-    return [dict(h=0, d=far[0], via=same[0], small=on[0:p], big=on[0:q], last=on[0:q]),
-            dict(h=0, d=far[1], via=same[1], small=on[p:q], big=on[q:], last=None),
-            dict(h=0, d=near[0], via=None, small=off[0:q], big=off, last=off),
-            dict(h=1, d=far[0], via=rest[0], small=on[q:q + p], big=on[0:q], last=None),
-            dict(h=1, d=far[1], via=rest[1], small=on[q + p:], big=on[q:], last=on[q:]),
-            dict(h=1, d=near[0], via=spare[0], small=off[q:], big=off[q:], last=None)]
+    return [dict(h=0, d=far[0], near=False, via=same[0], small=on[0:1], big=on, win=on[0:1], last=on),
+            dict(h=0, d=far[1], near=False, via=same[1], small=on[q:q + 1], big=off, win=on[q:q + 1], last=off),
+            dict(h=0, d=near[0], near=True, via=None, small=off[0:1], big=off, win=off[0:1], last=off),
+            dict(h=1, d=far[0], near=False, via=rest[0], small=on[2:3], big=on, win=None, last=None),
+            dict(h=1, d=far[1], near=False, via=rest[1], small=on[q + 2:q + 3], big=off, win=None, last=None),
+            dict(h=1, d=near[0], near=True, via=spare[0], small=off[2:3], big=on, win=None, last=None)]
 
 
 def relay_program(g, core, T, topo):
@@ -70,16 +74,14 @@ def relay_program(g, core, T, topo):
             h, dst = w["h"], T.cores[w["d"]]
             rid, pid = topo.addr(dst, core)
             m = topo.mask(core, dst)
-            n = len(topo.engines(core, dst))
-            g.wait_ge(T.sem.rsm, len(w["small"]))
-            g.remote_dma(T.ds[4 * h + c], T.rs[:], T.sem.asm, T.sem.sent, pid, rid, m)
-            g.wait_ge(T.sem.rbig, len(w["big"]))
-            g.remote_dma(T.db[4 * h + c], T.rb[:], T.sem["ab%d" % h], T.sem.sent, pid, rid, m)
-            tot = 2 * n
-            if w["last"]:
-                g.wait_ge(T.sem.rfin, len(w["last"]))
-                g.remote_dma(T.df[c], T.ro[:], T.sem.af, T.sem.sent, pid, rid, m)
-                tot += n
+            tot = 0
+            for kind, came, here, there, sem in (("small", "rsm", T.rs, T.ds[4 * h + c], "as%d" % h),
+                                                 ("big", "rbig", T.rb, T.db[4 * h + c], ("an%d" if w["near"] else "af%d") % h),
+                                                 ("win", "rwin", T.rw, T.dy[c], "ay"), ("last", "rlast", T.ro, T.df[c], "al")):
+                if w[kind]:
+                    g.wait_ge(T.sem[came], len(w[kind]))
+                    g.remote_dma(there, here[:], T.sem[sem], T.sem.sent, pid, rid, m)
+                    tot += len(topo.engines(core, dst))
             g.wait_ge(T.sem.sent, tot)
 
 
@@ -208,30 +210,40 @@ def rank_program(g, core, T, topo):
         before("g", reads.split(), [])
         g.remote_dma_fused(trs, local_sem=T.sem.sent)
 
-    def coming(kind, hs):
-        n = 0
+    def coming(kind, h=0, near=(True, False)):
+        who, n = [], 0
         for d in range(len(T.cores)):
             if d != c:
                 for w in routes(T, topo, d):
-                    if w["d"] == c and w["h"] in hs and w[kind]:
+                    if w["d"] == c and w["h"] == h and w["near"] in near and w[kind]:
+                        who.append(d)
                         n += len(w[kind]) if w["via"] is None else len(topo.engines(w["via"], core))
-        return n
-
-    dmas("a", "lsm", [(T.ssrc[:, 0:16], T.pa[:]), (T.ssrc[:, 16:17], T.w1[:]), (T.ssrc[:, 20:36], T.pb[:]), (T.ssrc[:, 36:37], T.w2[:])], "", "ssrc")
+        return who, n
 
     def xload(h, d, at):
         return (T.xi[:, at:at + 256], T.x[32 * d:32 * d + 32, 1024 * h:1024 * h + 1024])
-    dmas("s", "lx0", [xload(0, w["d"], 256 * k) for k, w in enumerate(ways[0:3])], "", "xi0")
-    dmas("a", "lx1", [xload(1, w["d"], 768 + 256 * k) for k, w in enumerate(ways[3:6])], "", "xi1")
-    dmas("a", "lxo", [xload(h, c, 1536 + 256 * h) for h in range(2)], "", "xi2")
+    dmas("s", "lw", [(T.st[:, 0:4, :], T.w1[:]), (T.st[:, 4:8, :], T.w2[:])], "", "su")
+    dmas("s", "lx0", [xload(0, w["d"], 256 * k) for k, w in enumerate(ways[0:2])], "", "xi0")
+    dmas("a", "lsm", [(T.st[:, 8:72, :], T.pa[:]), (T.st[:, 72:136, :], T.pb[:])], "", "st")
+    dmas("a", "lx2", [xload(1, w["d"], 768 + 256 * k) for k, w in enumerate(ways[3:5])], "", "xi2")
+    dmas("s", "lx1", [xload(0, ways[2]["d"], 512)], "", "xi1")
+    dmas("s", "lx3", [xload(1, ways[5]["d"], 1280)], "", "xi3")
 
     ms(T.kb[:], BIG, "kb")
     io(T.pi[:], [[32, 4]], 0, 1, "pi", True)
     io(T.jj[:], [[1, 144]], -15, 0, "jj")
     io(T.jg[:], [[16, 8], [0, 16]], 0, 0, "jg")
-    io(T.j32[:], [[0, 4], [1, 32]], 0, 0, "j32")
-    for k in (0, 1, 2, 3, 5):
-        op("a", lambda: act.activation(T.tab[:, V * k:V * k + V], T.kb[:], F.Silu), "kb", "tab%d" % k)
+    send(ways, "small", lambda w: T.st[w["d"], 8 * w["h"]:8 * w["h"] + 128, :], lambda w: T.ds[c], T.rs[:], ("as0", "rsm"), "su st")
+    dmas("s", "ow", [(T.ds[c, 0:72, :], T.st[c, 0:72, :])], "su st", "ds0")
+    dmas("s", "osm", [(T.ds[4 + c, 64:128, :], T.st[c, 72:136, :])], "st", "ds1")
+    FILL = 9
+    for k in range(FILL):
+        op("a", lambda: act.activation(T.tab[:, 1024 * k:1024 * k + 1024], T.kb[:], F.Silu), "kb", "tab%d" % k)
+    ms(T.tab[:, 1024 * FILL:1024 * FILL + 1024], BIG, "tab%d" % FILL)
+
+    def big(ks, reads):
+        send([ways[k] for k in ks], "big", lambda w: T.xb[:, 256 * ways.index(w):256 * ways.index(w) + 256], lambda w: T.db[4 * w["h"] + c], T.rb[:],
+             ("an0", "rbig"), reads)
 
     p = T.pi[:, 0:1]
     ts(T.ci[:, 0:4], T.pi[:], 112, None, A.bitwise_and, None, "pi", "ci0")
@@ -239,114 +251,136 @@ def rank_program(g, core, T, topo):
     ts(T.ci[:, 5:6], p, 31, None, A.bitwise_and, None, "pi", "ci2")
     ts(T.ci[:, 6:7], p, 3, 1, A.logical_shift_right, A.bitwise_and, "pi", "ci3")
     ts(T.ci[:, 7:8], p, 1, 7, A.logical_shift_right, A.bitwise_and, "pi", "ci4")
+    ts(T.ci[:, 8:9], p, 1, None, A.bitwise_and, None, "pi", "ci5")
+    ts(T.ci[:, 9:10], p, 4, 1, A.logical_shift_right, A.bitwise_and, "pi", "ci6")
+    ts(T.ci[:, 10:11], p, 5, None, A.logical_shift_right, None, "pi", "ci7")
+    ts(T.ci[:, 12:16], T.pi[:], 127, None, A.bitwise_and, None, "pi", "ci8")
+    cp(T.xb[:, 0:512], T.xi[:, 0:512], "xi0", "xb0")
+    big((0, 1), "xb0")
+    cp(T.cf[:, 0:11], T.ci[:, 0:11], "ci0 ci1 ci2 ci3 ci4 ci5 ci6 ci7", "cf")
+    cp(T.cf[:, 20:24], T.ci[:, 12:16], "ci8", "cfr")
+    cp(T.xb[:, 768:1280], T.xi[:, 768:1280], "xi2", "xb2")
+    big((3, 4), "xb2")
+    dmas("s", "lx4", [xload(0, c, 1536)], "xb2", "xi4")
+    dmas("s", "lx5", [xload(1, c, 1792)], "", "xi5")
+    cp(T.xb[:, 512:768], T.xi[:, 512:768], "xi1", "xb1")
+    cp(T.xb[:, 1280:1536], T.xi[:, 1280:1536], "xi3", "xb3")
+    big((2, 5), "xb1 xb3")
 
-    send(ways, "small", lambda w: T.ssrc[:, 20 * w["h"]:20 * w["h"] + 17], lambda w: T.ds[4 * w["h"] + c], T.rs[:], ("asm", "rsm"), "ssrc")
-    dmas("s", "osm", [(T.ds[4 * h + c], T.ssrc[:, 20 * h:20 * h + 17]) for h in range(2)], "ssrc", "ds")
-    for h in range(2):
-        cp(T.xb[:, 768 * h:768 * h + 768], T.xi[:, 768 * h:768 * h + 768], "xi%d" % h, "xb%d" % h)
-        send(ways[3 * h:3 * h + 3], "big", lambda w: T.xb[:, 256 * ways.index(w):256 * ways.index(w) + 256], lambda w: T.db[4 * h + c], T.rb[:],
-             ("ab%d" % h, "rbig"), "xb%d" % h)
-        if h == 0:
-            ts(T.ci[:, 8:9], p, 1, None, A.bitwise_and, None, "pi", "ci5")
-            ts(T.ci[:, 9:10], p, 4, 1, A.logical_shift_right, A.bitwise_and, "pi", "ci6")
-            ts(T.ci[:, 10:11], p, 5, None, A.logical_shift_right, None, "pi", "ci7")
-            cp(T.ci[:, 11:12], p, "pi", "ci8")
-    cp(T.xb[:, 1536:2048], T.xi[:, 1536:2048], "xi2", "xb2")
-    dmas("s", "ob", [(T.db[4 * h + c], T.xb[:, 1536 + 256 * h:1792 + 256 * h]) for h in range(2)], "xb2", "db0 db1")
-    arrives("asm", coming("small", (0, 1)), "ds")
-    arrives("ab0", coming("big", (0,)), "db0")
-    arrives("ab1", coming("big", (1,)), "db1")
-
+    def lay_in(h, sem, who, tag):
+        dmas("s", sem, [(T.xn[32 * r:32 * r + 32, 1024 * h:1024 * h + 1024], T.db[4 * h + r] if r != c else T.xb[:, 1536 + 256 * h:1792 + 256 * h])
+                        for r in who], tag, "x" + tag)
+    io(T.j32[:], [[0, 4], [1, 32]], 0, 0, "j32")
     io(T.jy[:], [[0, 4], [1, 2], [0, 16]], 0, 0, "jy")
     io(T.io8[:], [[16, 8]], 0, 0, "io8")
-    io(T.tab[:, 4 * V:5 * V], [[0, V]], int(BIG), 0, "tab4")
-
-    r0 = 32 * c
-    dmas("s", "gsm", [(T.sm[:, 0:17], T.ds[0:4, r0:r0 + 32, :]), (T.sm[:, 20:37], T.ds[4:8, r0:r0 + 32, :]),
-                      (T.smn[0:96, :], T.ds[1:4, r0:r0 + 32, 0:16]), (T.smn[96:128, :], T.ds[0, r0:r0 + 32, 0:16])], "ds", "sm")
-    for h in range(2):
-        dmas("s", "gx%d" % h, [(T.xn[:, 1024 * h:1024 * h + 1024], T.db[4 * h:4 * h + 4])], "db%d" % h, "xn%d" % h)
-    mv = []
-    for h in range(2):
-        mv += [(T.pn[32:128, 1024 * h:1024 * h + 1024], T.db[4 * h:4 * h + 3]), (T.pn[0:32, 1024 * h:1024 * h + 1024], T.db[4 * h + 3])]
-    dmas("s", "gp", mv, "db0 db1", "pn")
-    mv = []
-    for h in range(2):
-        mv += [(T.sn[0:96, 1024 * h:1024 * h + 1024], T.db[4 * h + 1:4 * h + 4]), (T.sn[96:128, 1024 * h:1024 * h + 1024], T.db[4 * h])]
-    dmas("s", "gs", mv, "db0 db1", "sn")
-
-    cp(T.cf[:, 0:12], T.ci[:], "ci0 ci1 ci2 ci3 ci4 ci5 ci6 ci7 ci8", "cf")
-    ms(T.msk[:, 8:16], 0.0, "msk2")
+    io(T.tab[:, TW - V:TW], [[0, V]], int(BIG), 0, "tab%d tab%d" % (FILL + 1, FILL + 2))
 
     def col(k):
         return T.cf[:, k:k + 1]
-    G0, G2, G6, C16, P31, HH, I2, ODD, YY, RK, PN = [col(k) for k in (0, 1, 3, 4, 5, 6, 7, 8, 9, 10, 11)]
-    ts(col(12), HH, 4.0, G6, A.mult, A.add, "cf", "c12")
-    ts(col(13), HH, 2.0, G2, A.mult, A.add, "cf", "c13")
+    G0, G2, G6, C16, P31, HH, I2, ODD, YY, RK, PN, P2, P6 = [col(k) for k in (0, 1, 3, 4, 5, 6, 7, 8, 9, 10, 20, 21, 23)]
+    J0 = T.jj[:, 15:143]
+    ts(T.shn[:], J0, P6, None, A.is_equal, None, "cfr jj", "shn")
+    ts(T.nshp[:], J0, P2, -1.0, A.is_equal, A.mult, "cfr jj", "nshp")
+    ts(T.idb[:], J0, PN, None, A.is_equal, None, "cfr jj", "idb")
+    ts(col(12), HH, 8.0, G6, A.mult, A.add, "cf", "c12")
+    ts(col(13), HH, 4.0, G2, A.mult, A.add, "cf", "c13")
     ts(col(14), I2, G0, None, A.add, None, "cf", "c14")
     ts(col(15), ODD, 511.0, 1.0, A.mult, A.add, "cf", "c15")
     ts(col(16), C16, 128.0, float(TW), A.mult, A.add, "cf", "c16")
     ts(col(17), RK, -1.0, 3.0, A.mult, A.add, "cf", "c17")
-    ts(col(18), HH, 2.0, G6, A.mult, A.add, "cf", "c18")
     ts(col(19), I2, G2, None, A.add, None, "cf", "c19")
-    J0 = T.jj[:, 15:143]
-    ts(T.rr[:], T.j32[:], P31, None, A.is_equal, None, "cf j32", "rr")
-    ts(T.zf[:], T.jj[:], G6, None, A.is_equal, None, "cf jj", "zf")
-    ts(T.zr[:], T.jj[:], G2, 16384.0, A.is_equal, A.mult, "cf jj", "zr")
-    ts(T.idb[:], J0, PN, None, A.is_equal, None, "cf jj", "idb")
-    ts(T.idf[:], J0, PN, None, A.is_equal, None, "cf jj", "idf")
-    ts(T.bg[:], T.jg[:], G0, -512.0, A.is_equal, A.mult, "cf jg", "bg")
-    ts(T.bgs[:], T.jg[:], G2, -512.0, A.is_equal, A.mult, "cf jg", "bgs")
-    ts(T.yf[:], T.jj[:], col(12), None, A.is_equal, None, "c12 jj", "yf")
-    ts(T.yh[:], T.jj[:], col(18), None, A.is_equal, None, "c18 jj", "yh")
-    ts(T.yr[:], T.jj[:], col(13), 16384.0, A.is_equal, A.mult, "c13 jj", "yr")
-    ts(T.kk[:], T.jj[:, 7:143], col(14), col(15), A.is_equal, A.mult, "c14 c15 jj", "kk")
+    ts(col(11), YY, 32.0, C16, A.mult, A.add, "cf", "c11")
     ts(T.k2[:], T.jj[:, 7:143], col(19), col(15), A.is_equal, A.mult, "c19 c15 jj", "k2")
-    ts(T.nid[:], J0, PN, -4096.0, A.is_equal, A.mult, "cf jj", "nid")
-    ms(T.mone[:], -1.0, "mone")
+    ts(T.idf[:], J0, PN, None, A.is_equal, None, "cfr jj", "idf")
+    ts(T.nid[:], J0, PN, -4096.0, A.is_equal, A.mult, "cfr jj", "nid")
+    ms(T.msk[:, 8:16], 0.0, "msk2")
     ms(T.crow[0:1, 0:4], -2047.5, "crow0")
     ms(T.crow[0:1, 4:7], 0.0, "crow1")
     ms(T.crow[0:1, 7:8], 2047.5, "crow2")
-    ts(T.off[:], J0, col(16), None, A.add, None, "c16 jj", "off")
-    ts(T.e16[:], T.jj[:, 15:31], C16, 1.0e9, A.not_equal, A.mult, "cf jj", "e16")
     ts(T.msk[:, 0:4], T.jj[:, 15:19], RK, None, A.is_equal, None, "cf jj", "msk0")
     ts(T.mtmp[:, 0:5], T.jj[:, 15:20], col(17), None, A.is_equal, None, "c17 jj", "mtmp")
-    ms(T.kr[0:2, :], 1024.0, "kr")
-    ts(T.e16[:], T.e16[:], float(TW), None, A.add, None, "e16", "e16")
+    ms(T.ks[:], 0, "ks")
+    ms(T.onef[0:1, :], 1.0, "onef")
     tt(T.msk[:, 4:8], T.mtmp[:, 0:4], T.mtmp[:, 1:5], A.subtract, "mtmp", "msk1")
+    ms(T.kr[0:2, :], 1024.0, "kr")
+    for h in range(2):
+        cp(T.xb[:, 1536 + 256 * h:1792 + 256 * h], T.xi[:, 1536 + 256 * h:1792 + 256 * h], "xi%d" % (4 + h), "xo%d" % h)
+        lay_in(h, "ob%d" % h, [c], "xo%d" % h)
+    ts(T.zf[:], T.jj[:], G6, None, A.is_equal, None, "cf jj", "zf")
+    ts(T.yf[:], T.jj[:], col(12), None, A.is_equal, None, "c12 jj", "yf")
+    ts(T.kk[:], T.jj[:, 7:143], col(14), col(15), A.is_equal, A.mult, "c14 c15 jj", "kk")
+    ts(T.e16[:], T.jj[:, 15:31], C16, 1.0e9, A.not_equal, A.mult, "cf jj", "e16")
+    ts(T.nk2[:], T.k2[:], -1.0, None, A.mult, None, "k2", "nk2")
+    ts(T.rr[:], T.j32[:], P31, None, A.is_equal, None, "cf j32", "rr")
+    ts(T.e16[:], T.e16[:], float(TW), None, A.add, None, "e16", "e16")
+    io(T.kr[0:1, :], [[1, 256]], 0, 0, "kr")
+    io(T.jw[:], [[1, 164]], -33, 0, "jw")
+    io(T.tab[:, TW:TD], [[0, V]], int(BIG), 0, "tabd")
+    for h in range(2):
+        arrives("as%d" % h, coming("small", h)[1], "ds%d" % h)
+        arrives("an%d" % h, coming("big", h, (True,))[1], "dn%d" % h)
+        arrives("af%d" % h, coming("big", h, (False,))[1], "df%d" % h)
+
+    dmas("s", "gw", [(T.wi[:, 4 * u:4 * u + 1], T.ds[0:4, 4 * u:4 * u + 4, :]) for u in range(2)], "ds0", "wi")
+    dmas("s", "gsm", [(T.sm[0:96, 16:32], T.ds[1:4, 8:72, :]), (T.sm[96:128, 16:32], T.ds[0, 8:72, :]), (T.sm[:, 0:16], T.ds[4:8, 64:128, :])], "ds0 ds1", "sm")
+    lay_in(0, "gx0", coming("big", 0, (False,))[0], "df0")
+    lay_in(0, "gy0", coming("big", 0, (True,))[0], "dn0")
+    lay_in(1, "gx1", coming("big", 1, (False,))[0], "df1")
+    lay_in(1, "gy1", coming("big", 1, (True,))[0], "dn1")
+    XH = ["xxo0 xdn0 xdf0", "xxo1 xdn1 xdf1"]
+    XA = XH[0] + " " + XH[1]
+    dmas("s", "gp", [(T.pn[32:128, :], T.xn[0:96, :]), (T.pn[0:32, :], T.xn[96:128, :])], XA, "pn")
+    dmas("s", "gs", [(T.sn[0:96, :], T.xn[32:128, :]), (T.sn[96:128, :], T.xn[0:32, :])], XA, "sn")
+
+    ts(T.sg[:], T.jy[:], YY, 4.0, A.is_equal, A.mult, "cf jy", "sg")
+    ms(T.mone[:], -1.0, "mone")
+    ts(T.off[:], J0, col(16), None, A.add, None, "c16 jj", "off0 off1")
     ms(T.dw[:, 0:3], 128.0, "dw0")
     ms(T.dw[:, 3:4], 0.0, "dw1")
-    ms(T.ks[:], 0, "ks")
+    ts(T.io8[:], T.io8[:], C16, None, A.add, None, "cf io8", "io8")
     ms(T.zer[:], 0.0, "zer")
     ms(T.dall[:, 256:272], NOD, "dall1")
     ms(T.oneb[0:2, :], 1.0, "oneb")
-    ms(T.onef[0:1, :], 1.0, "onef")
-    ms(T.qq[:], 4.0, "qq")
-    ts(T.sg[:], T.jy[:], YY, 4.0, A.is_equal, A.mult, "cf jy", "sg")
-    ts(T.io8[:], T.io8[:], C16, None, A.add, None, "cf io8", "io8")
-    io(T.kr[0:1, :], [[1, 256]], 0, 0, "kr")
-    io(T.tab[:, 6 * V:7 * V], [[0, V]], int(BIG), 0, "tab6")
-
-    cp(T.wf[:, 0:2], T.sm[:, 16:37:20], "sm", "wf")
-    ts(T.li[:, 0:16], T.sm[:, 20:36], 127, None, A.bitwise_and, None, "sm", "li0")
-    for u, z in enumerate((T.zw1, T.zw2)):
-        ts(z[:], T.jj[:], G0, T.wf[:, u:u + 1], A.is_equal, A.mult, "cf jj wf", "zw%d" % u)
+    ts(col(11), col(11), 2.0, None, A.mult, None, "c11", "c11")
+    ts(T.nkk[:], T.kk[:], -1.0, None, A.mult, None, "kk", "nkk")
+    ts(T.zr[:], T.jj[:], G2, 16384.0, A.is_equal, A.mult, "cf jj", "zr")
+    ts(T.yr[:], T.jj[:], col(13), 16384.0, A.is_equal, A.mult, "c13 jj", "yr")
+    ts(T.bg[:], T.jg[:], G0, -512.0, A.is_equal, A.mult, "cf jg", "bg")
+    ts(T.bgs[:], T.jg[:], G2, -512.0, A.is_equal, A.mult, "cf jg", "bgs")
+    cp(T.wf[:, 0:2], T.wi[:, 0:5:4], "wi", "wf")
+    cp(T.wfb[:], T.wi[:, 0:5:4], "wi", "wfb")
+    ZW, ZN, ZP = (T.zw0, T.zw1), (T.zn0, T.zn1), (T.zp0, T.zp1)
+    mm([(T.ka[:, 0:2], T.shn[:], T.wfb[:], True, True), (T.ka[:, 2:4], T.nshp[:], T.wfb[:], True, True)], "shn nshp wfb", "pska")
     for u in range(2):
-        ts(T.bw[:, 128 * u:128 * u + 128], T.jg[:], G0, T.wf[:, u:u + 1], A.is_equal, A.mult, "cf jg wf", "bw%d" % u)
+        ts(ZW[u][:], T.jj[:], G0, T.wf[:, u:u + 1], A.is_equal, A.mult, "cf jj wf", "zw%d" % u)
+    cp(T.wf[:, 4:8], T.ka[:, 0:4], "pska", "wfs")
+    ts(T.li[:, 32:64], T.sm[:], 6, 15, A.logical_shift_right, A.bitwise_and, "sm", "li1")
+    ts(T.bw[:, 0:128], T.jg[:], G0, T.wf[:, 0:1], A.is_equal, A.mult, "cf jg wf", "bw0")
+    cp(T.l7[:, 32:64], T.li[:, 32:64], "li1", "l7b")
+    ac(T.thr[:], T.e16[:, 0:16].indirect(T.l7[:, 32:64]), F.Identity, 0.0, 1.0, "e16 l7b", "thr")
+    ts(T.bw[:, 128:256], T.jg[:], G0, T.wf[:, 1:2], A.is_equal, A.mult, "cf jg wf", "bw1")
     mm([(T.ka[:, 0:256], T.rr[:], T.bw[:], True, True)], "rr bw0 bw1", "pska")
-    ts(T.li[:, 16:32], T.smn[:], 127, None, A.bitwise_and, None, "sm", "li1")
-    ts(T.li[:, 32:48], T.sm[:, 20:36], 7, None, A.logical_shift_right, None, "sm", "li2")
-    ts(T.li[:, 48:64], T.smn[:], 7, None, A.logical_shift_right, None, "sm", "li3")
-    cp(T.lp[:, 0:16], T.sm[:, 0:16], "sm", "lp0")
-    cp(T.lp[:, 16:32], T.sm[:, 20:36], "sm", "lp1")
-    cp(T.l7[:], T.li[:], "li0 li1 li2 li3", "l7")
-    ac(T.wm[:], T.ka[:, 0:256], F.Identity, 0.0, 1.0, "pska", "wm")
-    ac(T.thr[:], T.e16[:, 0:16].indirect(T.l7[:, 32:64]), F.Identity, 0.0, 1.0, "e16 l7", "thr")
-    for d in range(4):
-        ts(T.wm4[:, 128 * d:128 * d + 128], T.wm[:, 128:256], T.msk[:, d:d + 1], None, A.mult, None, "wm msk0", "wm4%d" % d)
+    for u in range(2):
+        ts(ZN[u][:], T.jj[:], G2, T.wf[:, 4 + u:5 + u], A.is_equal, A.mult, "cf jj wfs", "zn%d" % u)
+    cp(T.wm[:], T.ka[:, 0:256], "pska", "wm")
+    cp(T.lp[:], T.sm[:], "sm", "lp")
+    for u in range(2):
+        ts(ZP[u][:], T.jj[:], G6, T.wf[:, 6 + u:7 + u], A.is_equal, A.mult, "cf jj wfs", "zp%d" % u)
 
-    def places(k, n, u2, held, last, tags, out_tag):
-        a = 256 * k
+    def later():
+        return [lambda d=d: ts(T.wm4[:, 128 * d:128 * d + 128], T.wm[:, 128:256], T.msk[:, d:d + 1], None, A.mult, None, "wm msk0", "wm4%d" % d)
+                for d in range(4)]
+
+    def latest():
+        ts(T.li[:, 0:32], T.sm[:], 63, None, A.bitwise_and, None, "sm", "li0")
+        ts(T.li[:, 64:96], T.sm[:], 4, 64, A.logical_shift_right, A.bitwise_and, "sm", "li2")
+        tt(T.li[:, 0:32], T.li[:, 0:32], T.li[:, 64:96], A.add, "li0 li2", "li0")
+        cp(T.l7[:, 0:32], T.li[:, 0:32], "li0", "l7")
+
+    def result_rows(r):
+        ts(T.rl[:, 164 * r:164 * r + 164], T.jw[:], col(11), T.mtmp[:, 3 - r:4 - r], A.is_equal, A.mult, "c11 jw mtmp", "rl%d" % r)
+
+    def places(k, a, n, u2, held, last, tags, out_tag):
         u1, m = T.hs[:, a:a + n], T.hm[:, a:a + n]
         hs, hm = "hs_%d" % k, "hm_%d" % k
         return [lambda: ts(u1, u1, 4095, None, A.bitwise_and, None, tags, hs),
@@ -355,90 +389,174 @@ def rank_program(g, core, T, topo):
                 lambda: tt(m, m, u2, A.add, hm + " " + held, hm),
                 lambda: cp(last, m, hm, out_tag)]
 
-    ZW = (T.zw1, T.zw2)
     MB = (T.m0, T.m1, T.m2, T.m3)
     ST = (T.st0, T.st1)
+    PK = [((T.st0, "psst0"), (T.st1, "psst1"), (T.pq, "pspq"))[b] for b in PLAN["bank"]]
 
-    def lay(k):
-        o, i = T.xf[:, k::16], T.xn[:, 128 * k:128 * k + 128]
-        if k % 2 == 0 and k < 12:
-            ts(o, i, 128.0, None, A.add, None, "xn%d" % (k // 8), "xf%d" % k)
+    def pack(bank, src, at, w, kk=T.kk, first=True, last=True, gap=0):
+        b = at + (gap or w)
+        return [(bank[:, 0:w], kk[:, 8:136], src[:, at:at + w], first, False), (bank[:, 0:w], kk[:, 0:128], src[:, b:b + w], False, last)]
+    alone = [int(k[1:]) for k in PLAN["aq"].split() if k[0] == "e"]
+
+    def scatter(h, src, reads, more=""):
+        op("a", lambda: act.activation(T.tab[:, 0:TD if more else TW].indirect(T.kl[:, 64 * h:64 * h + 64]), src, F.Silu),
+           "kl%d " % h + reads, "tab " + more)
+
+    def own_sums(h, u):
+        a = 1024 * h
+        mm([(MB[h][:, 64 * u:64 * u + 64], ZW[u][:, 15 - k:143 - k], T.xn[:, a + 64 * k:a + 64 * k + 64], k == 0, k == 15) for k in range(16)],
+           "zw%d %s" % (u, XH[h]), "psm%d" % h)
+
+    def pred_sums(h, u):
+        a = 1024 * h
+        mm([(MB[2 + u][:, 0:64], ZN[u][:, 15 - k:143 - k], T.xn[:, a + k:a + 1024:16], k == 0, k == 15) for k in range(16)],
+           "zn%d %s" % (u, XH[h]), "psm%d" % (2 + u))
+
+    def pred_keep(h, u):
+        ts(T.up[:, 128 * u + 64 * h:128 * u + 64 * h + 64], MB[2 + u][:, 0:64], LIFT * u, None, A.add, None, "psm%d" % (2 + u), "up%d_%d" % (u, h))
+
+    def pred_pack(h):
+        mm(pack((T.pq, T.m1)[h], T.xn, 1024 * h, 512, T.k2), "k2 " + XH[h], ("pspq", "psm1")[h])
+
+    def pred_packed(h, a=0, b=512):
+        o, tag = T.pc[:, 512 * h + a:512 * h + b], "pc%d" % h
+        if h == 0:
+            ac(o, T.pq[:], F.Identity, 64.0 * 513, 1.0, "pspq", tag)
         else:
-            ac(o, i, F.Identity, 128.0, 1.0, "xn%d" % (k // 8), "xf%d" % k)
-    for h in range(2):
-        for u in range(2):
-            mm([(MB[u][:, 0:128], ZW[u][:, 15 - k:143 - k], T.xn[:, 128 * k:128 * k + 128], k == 0, k == 15) for k in range(8 * h, 8 * h + 8)],
-               "zw%d xn%d" % (u, h), "psm%d" % u)
-        for k in range(8 * h, 8 * h + 8):
-            lay(k)
+            ts(o, T.m1[:, a:b], 64.0 * 513, None, A.add, None, "psm1", tag)
 
-    def pack(bank, src, at, w, to=0, kk=T.kk):
-        return [(bank[:, to:to + w], kk[:, 8:136], src[:, at:at + w], True, False),
-                (bank[:, to:to + w], kk[:, 0:128], src[:, at + w:at + 2 * w], False, True)]
-    shapes = sorted(set((a, w) for d, a, w in PLAN["a"]), key=lambda s: (-s[1], s[0]))
-    pc_at, at = {}, 0
-    banks = ((T.st0, "psst0"), (T.st1, "psst1"), (T.pq, "pspq"), (T.m3, "psm3"))
-    for k, (a, w) in enumerate(shapes):
-        pc_at[a, w] = at
-        at += w
-        mm(pack(banks[k][0], T.xn, a, w, 0, T.k2), "k2 xn0 xn1", banks[k][1])
-    for k, (a, w) in enumerate(shapes):
-        ac(T.pc[:, pc_at[a, w]:pc_at[a, w] + w], banks[k][0][:, 0:w], F.Identity, 64.0 * 513, 1.0, banks[k][1], "pc%d_%d" % (a, w))
+    def lay(h, k):
+        a = 1024 * h
+        o, i = T.xf[:, a + k:a + 1024:16], T.xn[:, a + 64 * k:a + 64 * k + 64]
+        if h == 1:
+            ts(o, i, 128.0, None, A.add, None, XH[h], "xf%d_%d" % (h, k))
+        else:
+            ac(o, i, F.Identity, 128.0, 1.0, XH[h], "xf%d_%d" % (h, k))
+
+    def own_places(h):
+        u12, u1, u2, m = T.ph[:, 0:128], T.ph[:, 0:64], T.ph[:, 64:128], T.ph[:, 128:192]
+        return [lambda: cp(u12, MB[h][:, 0:128], "psm%d" % h, "ph"),
+                lambda: ts(u12, u12, 4095, None, A.bitwise_and, None, "ph", "ph"),
+                lambda: tt(m, u1, u2, A.mult, "ph", "pm"),
+                lambda: ts(m, m, 5, 8191, A.logical_shift_right, A.bitwise_and, "pm", "pm"),
+                lambda: tt(T.pos[:, 64 * h:64 * h + 64], m, u2, A.add, "ph pm", "pos%d" % h),
+                lambda: cp(T.kl[:, 64 * h:64 * h + 64], T.pos[:, 64 * h:64 * h + 64], "pos%d" % h, "kl%d" % h)]
+
+    def build(h):
+        op("a", lambda: act.activation(T.tab[:, 0:TW].indirect(T.kl[:, 64 * h:64 * h + 64]), T.xf[:, 1024 * h:1024 * h + 1024], F.Silu),
+           "kl%d " % h + " ".join("xf%d_%d" % (h, k) for k in range(16)), "tab " + " ".join("tab%d" % k for k in range(TW // 1024)))
+
+    def differences(a, b, bank, tag):
+        n = 16 * (b - a)
+        mm([(bank[:, 0:n], T.idb[:], T.dtmp[:, 0:n], True, False), (bank[:, 0:n], T.nshp[:], T.dtmp[:, 256:256 + n], False, True)],
+           "idb nshp dt0 dt1", tag)
+
+    def u2_start(hs):
+        for k in range(2):
+            mm([(ST[k][:, 128 * d + 64 * hs[0]:128 * d + 64 * hs[-1] + 64], T.idf[:], T.up[:, 128 + 64 * hs[0]:192 + 64 * hs[-1]], d == 0 and hs[0] == 0, False)
+                for d in range(2)], "idf up1_0 up1_%d" % hs[-1], "psst%d" % k)
+
     for u in range(2):
-        cp(T.hs[:, 128 * u:128 * u + 128], MB[u][:, 0:128], "psm%d" % u, "hs%d" % u)
-    for u in range(2):
-        mm([(MB[2 + u][:, 0:128], ZW[u][:, 15 - k:143 - k], T.pn[:, k::16], k == 0, k == 15) for k in range(16)], "zw%d pn" % u, "psm%d" % (2 + u))
-    ts(T.hs[:, 0:256], T.hs[:, 0:256], 4095, None, A.bitwise_and, None, "hs0 hs1", "hs_0")
-    tt(T.hm[:, 0:128], T.hs[:, 0:128], T.hs[:, 128:256], A.mult, "hs_0", "hm_0")
-    ts(T.hm[:, 0:128], T.hm[:, 0:128], 5, 8191, A.logical_shift_right, A.bitwise_and, "hm_0", "hm_0")
-    tt(T.pos[:], T.hm[:, 0:128], T.hs[:, 128:256], A.add, "hm_0 hs_0", "pos")
-    cp(T.kl[:], T.pos[:], "pos", "kl")
-    op("a", lambda: act.activation(T.tab[:, 0:TW].indirect(T.kl[:]), T.xf[:], F.Silu),
-       "kl " + " ".join("xf%d" % k for k in range(16)), "tab " + " ".join("tab%d" % k for k in range(6)))
-    cp(T.dtmp[:], T.pn[:, 0:V].indirect(T.lp[:, 0:16]), "pn lp0", "dtmp")
-    tt(T.dall[:, 0:256], T.xn[:, 0:V].indirect(T.lp[:, 16:32]), T.dtmp[:], A.subtract, "xn0 xn1 lp1 dtmp", "dall0")
+        own_sums(0, u)
+    pred_pack(0)
+    for k in range(16):
+        lay(0, k)
+    pred_packed(0)
+    for u in (1, 0):
+        pred_sums(0, u)
+    weave(own_places(0), later() + [lambda: pred_keep(0, 1)])
+    build(0)
+    pred_keep(0, 0)
+    u2_start((0,))
+    own_sums(1, 0)
+    for k in range(2):
+        cp(T.dtmp[:, 256 * k:256 * k + 32], T.xn[:, 0:V].indirect(T.lp[:, 16 * k:16 * k + 2]), XA + " lp", "dt%d" % k)
+    differences(0, 2, T.ka, "pska")
+    own_sums(1, 1)
+    steps = own_places(1)
+    fillers = [lambda k=k: lay(1, k) for k in range(6)]
+    for k in range(5):
+        fillers += [steps[k], lambda k=k: lay(1, 6 + 2 * k), lambda k=k: lay(1, 7 + 2 * k)]
+    fillers += steps[5:]
+
+    def fill(n):
+        for f in fillers[:n]:
+            f()
+        del fillers[:n]
+    fill(4)
+    cp(T.dall[:, 0:32], T.ka[:, 0:32], "pska", "dall0")
+    pred_sums(1, 1)
+    fill(2)
 
     tabw = T.tab[:, 0:TW]
-    UB, ub = T.st1, "psst1"
 
-    def u2_start():
-        mm([(UB[:, 128 * d:128 * d + 128], T.idf[:], T.up[:, 128:256], d == 0, False) for d in range(4)], "idf up1", ub)
+    def winner_out(t, a=0, b=6):
+        y, w128, m = T.yt[:, 4 * t:4 * t + 4], T.sw[:, 4 * t + 3:4 * t + 4], T.mk[:, t:t + 1]
+        for args in [(y[:, 0:1], w128, F.Identity, 0.25, 1.0 / 512, "sw%d" % t, "yt0"),
+                     (y[:, 1:2], w128, F.Identity, 1.0, 1.0 / 128, "sw%d" % t, "yt1"),
+                     (y[:, 2:3], m, F.Identity, y[:, 0:1], 0.25, "mk%d yt0" % t, "yt2"),
+                     (y[:, 3:4], y[:, 2:3], F.Sign, -1.0, 1.0, "yt2", "yt3"),
+                     (T.ryw[:, t:t + 1], y[:, 3:4], F.Identity, -1.0, y[:, 1:2], "yt3 yt1", "rw%d" % t),
+                     (T.ryw[:, 4 + t:5 + t], y[:, 3:4], F.Identity, -1.0, y[:, 2:3], "yt3 yt2", "rc%d" % t)][a:b]:
+            ac(*args)
+
+    def results(t, js, tag):
+        order = [w["d"] for w in ways[0:3]] + [c]
+        mm([(T.m3[:, 32 * k:32 * k + 32], T.rl[:, 164 * r + 33 - s:164 * r + 161 - s], T.cov[:, 128 * t + 32 * j:128 * t + 32 * j + 32],
+             t + j + k == 0, t == RO - 1 and j == 3 and k == 3)
+            for j, s in enumerate((0, 1, 32, 33)) if j in js for k, r in enumerate(order)], "rl0 rl1 rl2 rl3 " + tag, "psm3")
 
     for t in range(RO):
+        last = t == RO - 1
+        dwin, dtag = (T.dall[:, 0:32], "dall0") if t == 0 else (T.dall[:, 0:272], "dall0 dall1 dall2")
         mm([(T.ka[:, 16:24], T.onef[0:1, :], T.crow[0:1, :], True, False)], "onef crow0 crow1 crow2", "pska")
-        if t == 0:
-            cp(T.up[:, 0:128], T.m2[:, 0:128], "psm2", "up0")
-            ts(T.up[:, 128:256], T.m3[:, 0:128], LIFT, None, A.add, None, "psm3", "up1")
-        tt(T.dm[:], T.dall[:, 0:272].indirect(T.ks[:, 0:1]), T.msk[:], A.mult, "dall0 dall1 ks msk0 msk1 msk2", "dm")
+        tt(T.dm[:], dwin.indirect(T.ks[:, 0:1]), T.msk[:], A.mult, dtag + " ks msk0 msk1 msk2", "dm")
         mm([(T.ka[:, 16:24], T.wm[:, 128:256], T.dm[:, 0:8], False, True), (T.ka[:, 8:16], T.wm[:, 0:128], T.dm[:, 0:8], True, True),
             (T.ka[:, 0:8], T.rr[:], T.dm[:, 0:8], True, True)], "wm rr dm", "pska")
+        cp(T.dbc[:], dwin.indirect(T.ks[:]), dtag + " ks", "dbc")
         if t == 0:
-            u2_start()
-        cp(T.dbc[:], T.dall[:, 0:272].indirect(T.ks[:]), "dall0 dall1 ks", "dbc")
-        mm([(UB[:, 128 * d:128 * d + 128], T.wm4[:, 128 * d:128 * d + 128], T.dbc[:], False, False) for d in range(4)], "wm40 wm41 wm42 wm43 dbc", ub)
-        fill = []
-        cp(T.av[:], T.ka[:, 0:24], "pska", "av")
-        for d in range(4):
-            ts(T.kq[:, 128 * d:128 * d + 128], T.up[:, 128:256], T.av[:, 16 + d:17 + d], 1.0 / 4096, A.add, A.mult, "up1 av", "kq%d" % d)
-        mm([(UB[:], T.nid[:], T.kq[:], False, True)], "nid kq0 kq1 kq2 kq3", ub)
+            fill(4)
+            pred_keep(1, 1)
+            pred_sums(1, 0)
+            fill(len(fillers))
+            build(1)
+            u2_start((1,))
+        for k in range(2):
+            mm([(ST[k][:, 128 * d:128 * d + 128], T.wm4[:, 256 * k + 128 * d:256 * k + 128 * d + 128], T.dbc[:], False, False) for d in range(2)],
+               "wm4%d wm4%d dbc" % (2 * k, 2 * k + 1), "psst%d" % k)
         if t == 0:
-            for u in range(2):
-                mm([(MB[u][:, 0:128], ZW[u][:, 15 - k:143 - k], T.sn[:, k::16], k == 0, k == 15) for k in range(16)], "zw%d sn" % u, "psm%d" % u)
-                fill.append(lambda u=u: ts(T.us[:, 128 * u:128 * u + 128], MB[u][:, 0:128], LIFT * u, None, A.add, None, "psm%d" % u, "us%d" % u))
-        mm([(T.ka[:, 32:36], T.onef[0:1, :], T.jj[0:1, 15:19], True, False)], "onef jj", "pska")
+            pred_keep(1, 0)
+
+        def quotients(k):
+            def one(d):
+                ts(T.kq[:, 128 * d:128 * d + 128], T.up[:, 128:256], T.ka[:, 16 + d:17 + d], 1.0 / 4096, A.add, A.mult, "up1_0 up1_1 pska", "kq%d" % d)
+                if d % 2:
+                    mm([(ST[k][:, 0:256], T.nid[:], T.kq[:, 256 * k:256 * k + 256], False, True)], "nid kq%d kq%d" % (d - 1, d), "psst%d" % k)
+            return [lambda d=d: one(d) for d in (2 * k, 2 * k + 1)]
 
         def sums(k):
-            return [lambda d=d: ts(T.hs[:, 128 * d:128 * d + 128], T.up[:, 0:128], T.av[:, 8 + d:9 + d], None, A.add, None, "up0 av hs_%d" % k, "hs%d" % d)
-                    for d in (2 * k, 2 * k + 1)]
-        weave(sums(0))
-        if t > 0:
-            ts(T.cov[:], T.off[:], float(TW), None, A.is_lt, None, "off", "cov")
+            return [lambda d=d: ts(T.hs[:, 128 * d:128 * d + 128], T.up[:, 0:128], T.ka[:, 8 + d:9 + d], None, A.add, None,
+                                   "up0_0 up0_1 pska hs_%d" % k, "hs%d" % d) for d in (2 * k, 2 * k + 1)]
+        weave(quotients(0) + sums(0))
+        cp(T.av[:], T.ka[:, 0:24], "pska", "av")
+        first = places(0, 0, 256, ST[0][:, 0:256], "psst0", T.lf[:, 0:256], "hs0 hs1", "lf0")
+        second = places(1, 256, 256, ST[1][:, 0:256], "psst1", T.lf[:, 256:512], "hs2 hs3", "lf1")
+        weave(first[0:1] + sums(1) + first[1:2] + quotients(1))
+        if t == 0:
+            pred_pack(1)
+            for u in range(2):
+                mm([(T.pq[:, 128 * u:128 * u + 128], ZP[u][:, 15 - k:143 - k], T.xn[:, k::16], k == 0, k == 15) for k in range(16)], "zp%d %s" % (u, XA), "pspq")
+        else:
             for d in range(4):
-                mm([(MB[d][:, 0:128], T.idb[:], T.cov[:], True, False)], "idb cov", "psm%d" % d)
-        weave(places(0, 256, UB[:, 0:256], ub, T.lf[:, 0:256], "hs0 hs1", "lf0"),
-              [lambda: ts(T.ba[:], T.av[:, 0:4], -1.0, -64.0, A.mult, A.add, "av", "ba")] + sums(1))
-        weave(places(1, 256, UB[:, 256:512], ub, T.lf[:, 256:512], "hs2 hs3", "lf1"),
-              [lambda: ts(T.cd[:], T.av[:, 0:4], 128.0, None, A.add, None, "av", "cd")] + fill)
+                mm([(MB[d][:, 0:128], T.nid[:], T.cov[:, 128 * t - 128:128 * t], True, False)], "nid cov%d" % (t - 1), "psm%d" % d)
+        mm([(T.ka[:, 32:36], T.onef[0:1, :], T.jj[0:1, 15:19], True, False)], "onef jj", "pska")
+        weave(first[2:4], second[0:2])
+        ts(T.ba[:], T.av[:, 0:4], -1.0, -64.0, A.mult, A.add, "av", "ba")
+        weave(first[4:5] + second[2:3])
+        ts(T.cd[:], T.av[:, 0:4], 128.0, None, A.add, None, "av", "cd")
+        weave([lambda k=k: pred_packed(1, 256 * k, 256 * k + 256) for k in range(2)] if t == 0 else
+              [lambda: result_rows(t), lambda: result_rows(0) if t == 1 else
+               tt(T.cov[:, 0:128], T.cov[:, 0:128], T.cov[:, 128 * t - 128:128 * t], A.add, "cov0 cov%d" % (t - 1), "cov0")], second[3:5])
 
         begun = [t > 0] * 4
         left = [V] * 4
@@ -446,173 +564,191 @@ def rank_program(g, core, T, topo):
         def lst(d, a, n):
             return T.lf[:, 128 * d + a // 16:128 * d + (a + n) // 16]
 
-        def into(d, z, src, at, first, n, notes, tags):
-            calls = []
+        def blocks(bank, z, src, at, a, n, first, last):
+            h, k = a // 1024, a % 1024 // 64
+            return [(bank[:, 64 * h:64 * h + 64], z[:, 15 - k - b:143 - k - b], src[:, at + 64 * b:at + 64 * b + 64], first and b == 0, last and b == n - 1)
+                    for b in range(n)]
+
+        def into(d, z, src, at, a, n, notes, tags):
             left[d] -= notes
-            for b in range(n):
-                calls.append((MB[d][:, 0:128], z[:, 15 - first - b:143 - first - b], src[:, at + 128 * b:at + 128 * b + 128],
-                              not begun[d], left[d] == 0 and b == n - 1))
-                begun[d] = True
-            mm(calls, tags, "psm%d" % d)
+            mm(blocks(MB[d], z, src, at, a, n, not begun[d], left[d] == 0), tags, "psm%d" % d)
+            begun[d] = True
 
         def a_get(k, d, a, w):
-            ac(T.ab[:, 1024 * (k % 2):1024 * (k % 2) + 2 * w], tabw.indirect(lst(d, a, 2 * w)), F.Identity, T.ba[:, d:d + 1], 1.0,
-               "tab ba lf%d" % (d // 2), "ab%d" % (k % 2))
+            at = 1024 * (k % 3)
+            for j, (b, n) in enumerate([(a, 1024)] if w == 512 else [(a, w), (a + 512, w)]):
+                ac(T.ab[:, at + w * j:at + w * j + n], tabw.indirect(lst(d, b, n)), F.Identity, T.ba[:, d:d + 1], 1.0,
+                   "tab ba lf%d" % (d // 2), "ab%d ac%d" % (k % 3, k % 3) if n == 1024 else "a%s%d" % ("bc"[j], k % 3))
 
-        def a_pack(k, w):
-            mm(pack(ST[k % 2], T.ab, 1024 * (k % 2), w), "kk ab%d" % (k % 2), "psst%d" % (k % 2))
+        def a_pre(k, d, a, w):
+            mm(pack(PK[k][0], T.xn, a, w, T.nk2, True, False, 512), "nk2 " + XA, PK[k][1])
+
+        def a_pack(k, d, a, w):
+            mm(pack(PK[k][0], T.ab, 1024 * (k % 3), w, T.kk, k not in alone), "kk ab%d ac%d" % (k % 3, k % 3), PK[k][1])
+
+        def a_test(k, d, a, w):
+            ac(T.fc[:, 512 * (k % 3):512 * (k % 3) + w], PK[k][0][:, 0:w], F.Abs, -64.0 * 513, 1.0, PK[k][1], "fc%d" % (k % 3))
 
         def a_cmp(k, d, a, w):
-            tt(T.fc[:, 512 * (k % 2):512 * (k % 2) + w], ST[k % 2][:, 0:w], T.pc[:, pc_at[a, w]:pc_at[a, w] + w], A.not_equal,
-               "psst%d pc%d_%d" % (k % 2, a, w), "fc%d" % (k % 2))
+            at = a // 1024 * 512 + a % 1024
+            tt(T.fc[:, 512 * (k % 3):512 * (k % 3) + w], PK[k][0][:, 0:w], T.pc[:, at:at + w], A.not_equal,
+               "%s pc%d" % (PK[k][1], a // 1024), "fc%d" % (k % 3))
 
         def a_sum(k, d, a, w):
-            into(d, T.yf if w == 512 else T.yh, T.fc, 512 * (k % 2), a // 128, w // 128, 2 * w, "yf yh fc%d" % (k % 2))
+            into(d, T.yf, T.fc, 512 * (k % 3), a, w // 64, 2 * w, "yf fc%d" % (k % 3))
 
         def v_get(k, d, a, n):
-            tt(T.eb[:, 1024 * (k % 2):1024 * (k % 2) + n], tabw.indirect(lst(d, a, n)), T.pn[:, a:a + n], A.subtract,
-               "tab pn lf%d" % (d // 2), "eb%d" % (k % 2))
+            tt(T.eb[:, 1024 * (k % 3):1024 * (k % 3) + n], tabw.indirect(lst(d, a, n)), T.pn[:, a:a + n], A.subtract,
+               "tab pn lf%d" % (d // 2), "eb%d" % (k % 3))
 
         def v_cmp(k, d, a, n):
-            e = T.eb[:, 1024 * (k % 2):1024 * (k % 2) + n]
-            ts(e, e, T.cd[:, d:d + 1], None, A.not_equal, None, "cd eb%d" % (k % 2), "eb%d" % (k % 2))
+            e = T.eb[:, 1024 * (k % 3):1024 * (k % 3) + n]
+            ts(e, e, T.cd[:, d:d + 1], None, A.not_equal, None, "cd eb%d" % (k % 3), "eb%d" % (k % 3))
 
         def v_sum(k, d, a, n):
-            into(d, T.zf, T.eb, 1024 * (k % 2), a // 128, n // 128, n, "zf eb%d" % (k % 2))
+            into(d, T.zf, T.eb, 1024 * (k % 3), a, n // 64, n, "zf eb%d" % (k % 3))
 
         def count(d):
             op("a", lambda: act.activation(T.fit[:, 128 * d:128 * d + 128], MB[d][:, 0:128], F.Relu, bias=1.0, scale=-1.0,
                                            accum_out=T.cn[:, 3 - d:4 - d]), "psm%d" % d, "fit%d cn%d" % (d, d))
 
-        ev, full = [], [0.0] * 4
-        own = []
+        jobs = {}
+        for j, u in enumerate(PLAN["a"]):
+            test, w = "t%d" % j, u[2]
+            prev = ["t%d" % i for i in range(j) if PLAN["bank"][i] == PLAN["bank"][j]]
+            jobs["ag%d" % j] = ("a", ["pk%d" % (j - 3)], 2.7 * w + 60, a_get, (j,) + u)
+            if j in alone:
+                jobs["pr%d" % j] = ("p", prev + ["ag%d" % (j - 1)], 0.9 * w, a_pre, (j,) + u)
+            jobs["pk%d" % j] = ("p", prev + ["ag%d" % j, "pr%d" % j], 0.9 * w, a_pack, (j,) + u)
+            jobs[test] = ("a" if j in alone else "v", ["pk%d" % j, "as%d" % (j - 3)], 0.9 * w, a_test if j in alone else a_cmp, (j,) + u)
+            jobs["as%d" % j] = ("p", [test], 0.45 * w, a_sum, (j,) + u)
         for k, u in enumerate(PLAN["v"]):
-            own += [(u[2] * 1.56 + 60, v_get, k, u), (u[2] * 0.52 + 60, v_cmp, k, u)]
-        got, packed, cmpd = [], [], []
-        tv, j = PLAN["lag"], 0
-        while j < len(PLAN["a"]) or own:
-            if j < len(PLAN["a"]) and len(packed) == j:
-                while len(got) <= j:
-                    i = len(got)
-                    s0 = max(got[-1] if got else 0.0, packed[i - 2] if i >= 2 else 0.0)
-                    ev.append((s0, len(ev), a_get, (i,) + PLAN["a"][i]))
-                    got.append(s0 + PLAN["a"][i][2] * 3.12 + 60)
-                s0 = max(got[j], cmpd[j - 2] if j >= 2 else 0.0)
-                ev.append((s0, len(ev), a_pack, (j, PLAN["a"][j][2])))
-                packed.append(s0 + PLAN["a"][j][2] * 1.04 + 160)
-            if j < len(PLAN["a"]) and (packed[j] <= tv + 150 or not own):
-                d, a, w = PLAN["a"][j]
-                tv = max(tv, packed[j])
-                ev.append((tv, len(ev), a_cmp, (j, d, a, w)))
-                tv += w * 1.04 + 60
-                cmpd.append(tv)
-                ev.append((tv, len(ev), a_sum, (j, d, a, w)))
-                full[d] = max(full[d], tv + w * 0.52 + 80)
-                j += 1
-            else:
-                dur, fn, k, u = own.pop(0)
-                ev.append((tv, len(ev), fn, (k,) + u))
-                tv += dur
-                if fn is v_cmp:
-                    ev.append((tv, len(ev), v_sum, (k,) + u))
-                    full[u[0]] = max(full[u[0]], tv + u[2] * 0.52 + 80)
+            jobs["vg%d" % k] = ("v", ["vs%d" % (k - 3)], 1.35 * u[2] + 50, v_get, (k,) + u)
+            jobs["vc%d" % k] = ("v", ["vg%d" % k], 0.45 * u[2], v_cmp, (k,) + u)
+            jobs["vs%d" % k] = ("p", ["vc%d" % k], 0.45 * u[2], v_sum, (k,) + u)
         for d in range(4):
-            ev.append((full[d], len(ev), count, (d,)))
-        for e in sorted(ev, key=lambda e: e[0:2]):
-            e[2](*e[3])
+            jobs["n%d" % d] = ("a", ["as%d" % j for j, u in enumerate(PLAN["a"]) if u[0] == d] + ["vs%d" % k for k, u in enumerate(PLAN["v"]) if u[0] == d],
+                               130, count, (d,))
+        line = {"a": [{"g": "ag", "e": "t", "n": "n"}[k[0]] + k[1:] for k in PLAN["aq"].split()],
+                "v": [{"g": "vg", "c": "vc", "p": "t"}[k[0]] + k[1:] for k in PLAN["vq"].split()]}
+        free, done = {"a": 0.0, "v": PLAN["lag"], "p": 0.0}, {}
+        while len(done) < len(jobs):
+            can = [k for k in line["a"][:1] + line["v"][:1] + [k for k in jobs if jobs[k][0] == "p" and k not in done]
+                   if all(x in done for x in jobs[k][1] if x in jobs)]
+            when = {k: max([free[jobs[k][0]]] + [done[x] + 100 for x in jobs[k][1] if x in jobs]) for k in can}
+            k = min(can, key=lambda k: (when[k] - (PLAN["ahead"] if k[:2] == "pk" else 0), k))
+            at = when[k]
+            q, _, ns, fn, args = jobs[k]
+            fn(*args)
+            free[q] = done[k] = at + ns
+            if q != "p":
+                line[q].pop(0)
+            if t == 0 and k == "ag1":
+                for u in range(2):
+                    ac(T.us[:, 128 * u:128 * u + 128], T.pq[:, 128 * u:128 * u + 128], F.Identity, LIFT * u, -1.0, "pspq", "us%d" % u)
 
-        if t > 0:
-            tt(T.qq[:], T.qq[:], T.cov[:], A.subtract, "qq cov", "qq")
-        mm([(T.ka[:, 32:36], T.sg[:], T.cn[:], False, True)], "sg cn0 cn1 cn2 cn3", "pska")
-        mm([(T.pq[:, 0:128], T.idf[:], T.us[:, 128:256], True, False)], "idf us1", "pspq")
         if t == 0:
-            mm(pack(ST[0], T.sn, 0, 256) + pack(ST[0], T.sn, 512, 256, 256), "kk sn", "psst0")
-        m = T.mk[:, t:t + 1]
-        op("v", lambda: vec.tensor_reduce(m, T.ka[:, 32:36], AxisListType.X, A.max), "pska", "mk")
-        ts(T.ns[:], T.ka[:, 32:36], m, None, A.not_equal, None, "pska mk", "ns")
+            latest()
 
-        def pick(k, src):
-            op("v", lambda: vec.tensor_tensor_scan(T.sel[:, 4 * k:4 * k + 4], T.ns[:], src, 0.0, A.mult, A.add), "ns av dw0 dw1", "sel%d" % k)
-        pick(2, T.av[:, 4:8])
-        pick(1, T.av[:, 20:24])
-        pick(0, T.av[:, 12:16])
-        W, w128 = T.sel[:, 11:12], T.sel[:, 15:16]
+        mm([(T.ka[:, 32:36], T.sg[:], T.cn[:], False, True)], "sg cn0 cn1 cn2 cn3", "pska")
+        if t == 0:
+            for k in range(2):
+                ac(T.dtmp[:, 256 * k:256 * k + 224], T.xn[:, 0:V].indirect(T.lp[:, 16 * k + 2:16 * k + 16]), F.Identity, 0.0, 1.0, XA + " lp", "dt%d" % k)
+        else:
+            winner_out(t - 1)
+        mm([(T.pq[:, 0:128], T.idf[:], T.us[:, 128:256], True, False)], "idf us1", "pspq")
+        if t == RO - 1:
+            results(0, (0, 1, 2, 3), "cov0")
+        m = T.mk[:, t:t + 1]
+        op("v", lambda: vec.tensor_reduce(m, T.ka[:, 32:36], AxisListType.X, A.max), "pska", "mk%d" % t)
+        ts(T.ns[:], T.ka[:, 32:36], m, None, A.not_equal, None, "pska mk%d" % t, "ns")
+
+        def pick(out, src, tag):
+            op("v", lambda: vec.tensor_tensor_scan(out, T.ns[:], src, 0.0, A.mult, A.add), "ns av dw0 dw1", tag)
+        pick(T.sel[:, 8:12], T.av[:, 4:8], "sel2")
+        pick(T.sel[:, 4:8], T.av[:, 20:24], "sel1")
+        pick(T.sel[:, 0:4], T.av[:, 12:16], "sel0")
+        W, w128 = T.sel[:, 11:12], T.sw[:, 4 * t + 3:4 * t + 4]
         ac(T.dbc[:], T.mone[:], F.Identity, 0.0, W, "mone sel2", "dbc")
         mm([(T.pq[:, 0:128], T.bw[:, 128:256], T.dbc[:], False, False)], "bw1 dbc", "pspq")
+        pick(T.sw[:, 4 * t:4 * t + 4], T.dw[:], "sw%d" % t)
         ts(T.kq[:, 0:128], T.us[:, 128:256], T.sel[:, 7:8], 1.0 / 4096, A.subtract, A.mult, "us1 sel1", "kq0")
         mm([(T.pq[:, 0:128], T.nid[:], T.kq[:, 0:128], False, True)], "nid kq0", "pspq")
-        for d in range(2):
-            mm([(MB[d][:, 0:128], T.idf[:], T.pos[:], True, False)], "idf pos", "psm%d" % d)
-        ts(T.hs[:, 0:128], T.us[:, 0:128], T.sel[:, 3:4], None, A.subtract, None, "us0 sel0 hs_0", "hs0")
-        pick(3, T.dw[:])
-        weave(places(0, 128, T.pq[:, 0:128], "pspq", T.lr[:], "hs0", "lr"),
-              [lambda: ts(T.ofw[:], T.io8[:], T.sel[:, 15:16], None, A.add, None, "io8 sel3", "ofw")])
+        for h in range(2):
+            ts(T.hs[:, 64 * h:64 * h + 64], T.us[:, 64 * h:64 * h + 64], T.sel[:, 3:4], None, A.subtract, None, "us0 sel0 hs_0 hs_1 hs0", "hw%d" % h)
+        weave(places(0, 0, 64, T.pq[:, 0:64], "pspq", T.lr[:, 0:64], "hw0", "lr0"),
+              places(1, 64, 64, T.pq[:, 64:128], "pspq", T.lr[:, 64:128], "hw1", "lr1"),
+              [lambda: ts(T.ofw[:], T.io8[:], w128, None, A.add, None, "io8 sw%d" % t, "ofw")])
+        BK = (T.m0, T.m2)
+        for h in range(2):
+            mm(pack(ST[h], T.sn, 1024 * h, 256, T.nkk, True, False), "nkk sn", "psst%d" % h)
+            if not last:
+                mm([(BK[h][:, 64 * h:64 * h + 64], T.idf[:], T.pos[:, 64 * h:64 * h + 64], True, False)], "idf pos%d" % h, "psm%d" % (2 * h))
+        mm([(T.m1[:, 0:128], T.idf[:], T.pos[:], True, False)], "idf pos0 pos1", "psm1")
         ac(T.br[:, 0:1], W, F.Identity, -64.0, 1.0, "sel2", "br")
-        ac(T.br[:, 1:2], W, F.Identity, -128.0, 1.0, "sel2", "br1")
         ac(T.cr[:, 0:1], W, F.Identity, 128.0, -1.0, "sel2", "cr")
-        if t == 0:
-            ac(T.sc[:], ST[0][:], F.Identity, 64.0 * 513, 1.0, "psst0", "sc0 sc1")
+        if last:
+            winner_out(t, 0, 3)
         ac(T.nf[:], T.fit[:, 0:512].indirect(T.ofw[:]), F.Identity, 16384.0, -16384.0, "fit0 fit1 fit2 fit3 ofw", "nf")
         mm([(T.m1[:, 0:128], T.idb[:], T.nf[:], False, True)], "idb nf", "psm1")
-        ac(T.yt[:, 0:1], w128, F.Identity, 0.25, 1.0 / 512, "sel3", "yt0")
-        ac(T.yt[:, 1:2], w128, F.Identity, 1.0, 1.0 / 128, "sel3", "yt1")
+        if last:
+            winner_out(t, 3, 6)
+            tags = " ".join("rw%d rc%d" % (k, k) for k in range(RO))
+            dmas("s", "oy", [(T.dy[c], T.ryw[0:32, :])], tags, "dy")
+            send(ways[0:3], "win", lambda w: T.dy[c], lambda w: T.dy[c], T.rw[:], ("ay", "rwin"), "dy")
 
-        def r_get(k):
-            ac(T.ab[:, 512 * k:512 * k + 512], tabw.indirect(T.lr[:, 32 * k:32 * k + 32]), F.Identity, T.br[:, 0:1], 1.0,
-               "tab lr br", "ar0 ab0" if k == 0 else "ar1")
-
-        def r_pack(k):
-            mm(pack(ST[k], T.ab, 512 * k, 256), "kk ar%d ab0" % k, "psst%d" % k)
-
-        def r_cmp(k):
-            tt(T.fc[:, 512 * k:512 * k + 256], ST[k][:, 0:256], T.sc[:, 256 * k:256 * k + 256], A.not_equal, "psst%d sc%d" % (k, k), "fc%d" % k)
-
-        def r_sum(k):
-            mm([(T.m0[:, 0:128], T.yr[:, 15 - 4 * k - b:143 - 4 * k - b], T.fc[:, 512 * k + 128 * b:512 * k + 128 * b + 128], False, k == 1 and b == 1)
-                for b in range(2)], "yr fc%d" % k, "psm0")
-
-        def z_sum(k):
-            mm([(T.m0[:, 0:128], T.zr[:, 7 - 4 * k - b:135 - 4 * k - b], T.eb[:, 1024 * k + 128 * b:1024 * k + 128 * b + 128], False, False)
-                for b in range(4)], "zr eb%d" % k, "psm0")
-        e0, e1 = T.eb[:, 0:512], T.eb[:, 1024:1536]
-        r_get(0)
-        tt(e0, tabw.indirect(T.lr[:, 64:96]), T.sn[:, 1024:1536], A.subtract, "tab lr sn", "eb0")
-        r_pack(0)
-        r_get(1)
-        tt(e1, tabw.indirect(T.lr[:, 96:128]), T.sn[:, 1536:2048], A.subtract, "tab lr sn", "eb1")
-        r_pack(1)
-        ac(e0, e0, F.Abs, T.br[:, 1:2], 1.0, "br1 eb0", "eb0")
-        r_cmp(0)
-        r_sum(0)
-        ts(e1, e1, T.cr[:, 0:1], None, A.not_equal, None, "cr eb1", "eb1")
-        z_sum(0)
-        r_cmp(1)
-        z_sum(1)
-        tt(T.bb[:], T.m1[:, 0:128], T.off[:], A.min, "psm1 off", "bb")
-        r_sum(1)
-        ac(T.yt[:, 2:3], m, F.Identity, T.yt[:, 0:1], 0.25, "mk yt0", "yt2")
-        ac(T.yt[:, 3:4], T.yt[:, 2:3], F.Sign, -1.0, 1.0, "yt2", "yt3")
-        ac(T.res[:, 128 + t:129 + t], T.yt[:, 3:4], F.Identity, -1.0, T.yt[:, 1:2], "yt3 yt1", "rw%d" % t)
-        ac(T.res[:, 132 + t:133 + t], T.yt[:, 3:4], F.Identity, -1.0, T.yt[:, 2:3], "yt3 yt2", "rc%d" % t)
-        tt(T.off[:], T.m0[:, 0:128], T.bb[:], A.min, "psm0 bb", "off")
-        if t < RO - 1:
-            cp(T.kl[:], T.off[:], "off", "kl")
-            u2_start()
-            op("a", lambda: act.activation(T.tab[:, 0:TD].indirect(T.kl[:]), T.kb[:], F.Silu), "kl kb", "tab tab6")
+        for h in range(2):
+            ac(T.ab[:, 1024 * h:1024 * h + 512], tabw.indirect(T.lr[:, 64 * h:64 * h + 32]), F.Identity, T.br[:, 0:1], 1.0, "tab lr%d br" % h, "ab%d ac%d" % (h, h))
+            mm(pack(ST[h], T.ab, 1024 * h, 256, T.kk, False, True), "kk ab%d" % h, "psst%d" % h)
+            tt(T.eb[:, 1024 * h:1024 * h + 512], tabw.indirect(T.lr[:, 64 * h + 32:64 * h + 64]), T.sn[:, 1024 * h + 512:1024 * h + 1024], A.subtract,
+               "tab lr%d sn" % h, "eb%d" % h)
+            e = T.eb[:, 1024 * h:1024 * h + 512]
+            if h == 0:
+                tt(T.bb[:], T.m1[:, 0:128], T.off[:], A.min, "psm1 off0 off1", "bb")
+            elif last:
+                ts(T.cov[:, 128:256], T.bb[:], float(TW), -2.0 ** 60, A.is_lt, A.mult, "bb", "cov1")
+            ts(e, e, T.cr[:, 0:1], None, A.not_equal, None, "cr eb%d" % h, "eb%d" % h)
+            if h == 0:
+                mm(blocks(BK[0], T.zr, T.eb, 0, 512, 8, last, False), "zr eb0", "psm0")
+        for h in range(2):
+            ac(T.fc[:, 512 * h:512 * h + 256], ST[h][:, 0:256], F.Abs, -64.0 * 513, 1.0, "psst%d" % h, "fc%d" % h)
+            if h == 1:
+                mm(blocks(BK[1], T.zr, T.eb, 1024, 1536, 8, last, False), "zr eb1", "psm2")
+            if last:
+                mm([(BK[h][:, 64 * h:64 * h + 64], T.idb[:], T.cov[:, 128 + 64 * h:192 + 64 * h], False, False)], "idb cov1", "psm%d" % (2 * h))
+            mm(blocks(BK[h], T.yr, T.fc, 512 * h, 1024 * h, 4, False, True), "yr fc%d" % h, "psm%d" % (2 * h))
+            if last:
+                ts(T.cov[:, 384 + 64 * h:448 + 64 * h], BK[h][:, 64 * h:64 * h + 64], 0.5, float(RO), A.is_lt, A.mult, "psm%d" % (2 * h), "cov3_%d" % h)
+            else:
+                o = T.off[:, 64 * h:64 * h + 64]
+                tt(o, BK[h][:, 64 * h:64 * h + 64], T.bb[:, 64 * h:64 * h + 64], A.min, "psm%d bb" % (2 * h), "off%d" % h)
+                cp(T.kl[:, 64 * h:64 * h + 64], o, "off%d" % h, "kl%d" % h)
+        if not last:
+            for h in range(2):
+                scatter(h, T.kb[:], "kb", "tabd")
+            u2_start((0, 1))
             mm([(T.pq[:, 0:256], T.oneb[0:2, :], T.kr[0:2, :], True, False)], "oneb kr", "pspq")
-            tt(T.pf[:], T.off[:, 0:128].indirect(T.l7[:, 0:32]), T.thr[:], A.is_ge, "off l7 thr", "pf")
+            if t == 0:
+                differences(2, 16, T.m3, "psm3")
+            tt(T.pf[:], T.off[:, 0:128].indirect(T.l7[:, 0:32]), T.thr[:], A.is_ge, "off0 off1 l7 thr", "pf")
             mm([(T.pq[:, 0:256], T.bg[:], T.pf[:, 0:256], False, False), (T.pq[:, 0:256], T.bgs[:], T.pf[:, 256:512], False, True)],
                "bg bgs pf", "pspq")
+            ts(T.cov[:, 128 * t:128 * t + 128], T.off[:], float(TW), -1.0, A.is_lt, A.mult, "off0 off1", "cov%d" % t)
+            if t == 0:
+                cp(T.dall[:, 32:256], T.m3[:, 0:224], "psm3", "dall2")
             op("v", lambda: vec.tensor_reduce(T.kmin[:, 0:1], T.pq[:, 0:256], AxisListType.X, A.min), "pspq", "kmin")
             ts(T.ks[:], T.zer[:], T.kmin[:, 0:1], float(PP), A.add, A.min, "kmin zer", "ks")
 
-    ts(T.bt[:], T.off[:], float(TW), None, A.is_lt, None, "off", "bt")
-    tt(T.res[:, 0:128], T.bt[:], T.qq[:], A.mult, "bt qq", "res")
-    tags = "res " + " ".join("rw%d rc%d" % (t, t) for t in range(RO))
-    send([w for w in ways if w["last"]], "last", lambda w: T.res[:], lambda w: T.df[c], T.ro[:], ("af", "rfin"), tags)
-    dmas("s", "of", [(T.df[c], T.res[:])], tags, "df")
-    arrives("af", coming("last", (0, 1)), "df")
-    dmas("s", "fin", [(T.yc[:], T.df[:, r0:r0 + 32, 0:128]), (T.yw[:], T.df[:, 0:32:16, 128:136])], "df", "")
+    for h in range(2):
+        results(RO - 1, (2 * h, 2 * h + 1), "cov3_%d" % h)
+    cp(T.res[:], T.m3[:, 0:128], "psm3", "res")
+    for ws in (ways[0:2], ways[2:3]):
+        send(ws, "last", lambda w: T.res[:, 32 * ways.index(w):32 * ways.index(w) + 32], lambda w: T.df[c], T.ro[:], ("al", "rlast"), "res")
+    dmas("s", "of", [(T.df[c], T.res[:, 96:128])], "res", "df")
+    arrives("ay", coming("win")[1], "dy")
+    arrives("al", coming("last")[1], "df")
+    dmas("a", "fiy", [(T.yw[y:8:2, :], T.dy[:, 64 * y:64 * y + 4, :]) for y in range(2)], "dy", "")
+    dmas("s", "fin", [(T.yc[:], T.df[:])], "df", "")
     cnt["sent"] = sent[0]
     for s in cnt:
         if seen.get(s, 0) < cnt[s]:

from concourse.bass import DstId, RemoteDMATransfer
from concourse.mybir import AluOpType, AxisListType, ActivationFunctionType

V, PP, RO = 2048, 256, 4
TW = 12288
TD = TW + V
BIG = 4000.0
NOD = -300.0
LIFT = 192.0 * 4096
PLAN = {"a": [(0, 0, 512), (0, 1024, 512), (1, 0, 512), (1, 1024, 512), (2, 0, 384), (2, 384, 128)],
        "v": [(3, 0, 1024), (3, 1024, 512), (3, 1536, 512), (2, 1024, 512), (2, 1536, 512)],
        "bank": [0, 1, 0, 1, 2, 0],
        "aq": "g0 g1 g2 g3 g4 g5 e4 n0 n3 n1 n2", "vq": "g0 c0 g1 p0 c1 g2 p1 c2 g3 p2 c3 g4 p3 c4 p5", "lag": 200.0, "ahead": 0.0}

F32, BF, I32, U16 = "float32", "bfloat16", "int32", "uint16"
SCRATCH = {}
for _dt, _bufs in (
    (F32, dict(tab=TD, kb=1024, xf=V, pc=1536, crow=8, zer=8, up=256, us=256, pos=128, off=128, bb=128, fit=512, thr=512,
               mtmp=8, av=24, ba=4, cn=4, mk=4, ns=4, sel=12, sw=16, dw=4, br=4, yt=16, kmin=4, io8=8, res=128, ryw=8, wf=8, jj=144, jw=164,
               j32=128, jg=128, jy=128, cf=28, idf=128, sg=128, e16=16, onef=128)),
    (BF, dict(xb=V, xn=V, pn=V, sn=V, ab=3072, eb=3072, fc=1536, kq=512, dbc=128, mone=128, nid=128, wm4=512, k2=136, nk2=136, nf=128, cov=512, pf=512,
              dall=272, dtmp=512, dm=16, msk=16, cd=4, cr=2, zf=144, zr=144, yf=144, yh=144, yr=144, zw0=144, zw1=144, zn0=144, zn1=144,
              zp0=144, zp1=144, kk=136, nkk=136, idb=128, rr=128, bg=128, bgs=128, bw=256, wm=256, kr=256, oneb=128, shn=128, nshp=128,
              wfb=2, rl=4 * 164)),
    (I32, dict(xi=V, hs=512, hm=512, ph=192, sm=32, wi=8, li=96, pi=4, ci=16)),
    (U16, dict(lf=512, lr=128, kl=128, ks=8, ofw=8, l7=64, lp=32)),
):
    for _k, _n in _bufs.items():
        SCRATCH[_k] = ("sbuf", [128, _n], _dt)
SCRATCH.update({"st": ("dram", [4, 136, 8], I32), "rs": ("dram", [128, 8], I32), "ds": ("dram", [8, 128, 8], I32),
                "rb": ("dram", [128, 256], BF), "db": ("dram", [8, 128, 256], BF),
                "rw": ("dram", [128, 2], F32), "dy": ("dram", [4, 128, 2], F32),
                "ro": ("dram", [128, 32], F32), "df": ("dram", [4, 128, 32], F32)})
for _k in ("m0", "m1", "m2", "m3", "st0", "st1", "ka", "pq"):
    SCRATCH[_k] = ("psum", [128, 512], F32)
SEMAPHORES = ["cv", "ca", "cp", "cg", "lw", "ow", "as0", "as1", "lsm", "lx0", "lx1", "lx2", "lx3", "lx4", "lx5", "osm", "ob0", "ob1", "gw", "gsm", "gx0", "gx1", "gy0", "gy1",
              "gp", "gs", "of", "oy", "fin", "fiy", "an0", "an1", "af0", "af1", "ay", "al", "rsm", "rbig", "rwin", "rlast", "sent"]


def bits(engs):
    m = 0
    for e in engs:
        m |= 1 << e
    return m


def routes(T, topo, c):
    n = len(T.cores)
    me = T.cores[c]
    others = [(c + k) % n for k in range(1, n)]
    near = [d for d in others if topo.may_write(me, T.cores[d])]
    far = [d for d in others if d not in near]
    chip = [k for k in topo.cores_of(me) if k not in T.cores]
    able = [k for k in chip if all(topo.may_write(k, T.cores[d]) for d in far)]
    same = [k for k in able if topo.die(k) == topo.die(me)]
    rest = [k for k in able if topo.die(k) != topo.die(me)]
    spare = [k for k in chip if k not in able and topo.die(k) != topo.die(me) and topo.may_write(k, T.cores[near[0]])]
    off = topo.engines(me, T.cores[near[0]])
    on = [e for e in topo.engines(me, same[0]) if e not in off]
    q = len(on) // 2
    return [dict(h=0, d=far[0], near=False, via=same[0], small=on[0:1], big=on, win=on[0:1], last=on),
            dict(h=0, d=far[1], near=False, via=same[1], small=on[q:q + 1], big=off, win=on[q:q + 1], last=off),
            dict(h=0, d=near[0], near=True, via=None, small=off[0:1], big=off, win=off[0:1], last=off),
            dict(h=1, d=far[0], near=False, via=rest[0], small=on[2:3], big=on, win=None, last=None),
            dict(h=1, d=far[1], near=False, via=rest[1], small=on[q + 2:q + 3], big=off, win=None, last=None),
            dict(h=1, d=near[0], near=True, via=spare[0], small=off[2:3], big=on, win=None, last=None)]


def relay_program(g, core, T, topo):
    for c in range(len(T.cores)):
        for w in routes(T, topo, c):
            if w["via"] != core:
                continue
            h, dst = w["h"], T.cores[w["d"]]
            rid, pid = topo.addr(dst, core)
            m = topo.mask(core, dst)
            tot = 0
            for kind, came, here, there, sem in (("small", "rsm", T.rs, T.ds[4 * h + c], "as%d" % h),
                                                 ("big", "rbig", T.rb, T.db[4 * h + c], ("an%d" if w["near"] else "af%d") % h),
                                                 ("win", "rwin", T.rw, T.dy[c], "ay"), ("last", "rlast", T.ro, T.df[c], "al")):
                if w[kind]:
                    g.wait_ge(T.sem[came], len(w[kind]))
                    g.remote_dma(there, here[:], T.sem[sem], T.sem.sent, pid, rid, m)
                    tot += len(topo.engines(core, dst))
            g.wait_ge(T.sem.sent, tot)


def rank_program(g, core, T, topo):
    c = T.rank_of(core)
    if c is None:
        relay_program(g, core, T, topo)
        return
    A, F = AluOpType, ActivationFunctionType
    Q = {"v": g.vector, "a": g.scalar, "p": g.tensor, "g": g, "s": g.sync}
    vec, act, pe = g.vector, g.scalar, g.tensor

    know = {q: {} for q in Q}
    snap, cnt, wr, rd, seen = {}, {}, {}, {}, {}

    def need(q, tok):
        s, n = tok
        if know[q].get(s, 0) >= n:
            return
        Q[q].wait_ge(T.sem[s], n)
        seen[s] = max(seen.get(s, 0), n)
        know[q][s] = n
        for k, m in snap.get(tok, {}).items():
            if know[q].get(k, 0) < m:
                know[q][k] = m

    def before(q, reads, writes):
        toks = []
        for t in reads:
            if t.startswith("ps"):
                continue
            toks += wr.get(t, [])
        for t in writes:
            if not t.startswith("ps"):
                toks += wr.get(t, []) + rd.get(t, [])
        for t in reads + writes:
            if t.startswith("ps"):
                toks += [k for k in wr.get(t, []) if k[0] != "c" + q]
        top = {}
        for s, n in toks:
            top[s] = max(top.get(s, 0), n)
        for s in sorted(top, key=lambda k: k == "c" + q):
            need(q, (s, top[s]))

    def after(tok, reads, writes):
        for t in reads:
            if t.startswith("ps"):
                wr[t] = [tok]
            else:
                rd.setdefault(t, []).append(tok)
        for t in writes:
            wr[t] = [tok]
            rd[t] = []

    def op(q, fn, reads, writes):
        reads, writes = reads.split(), writes.split()
        before(q, reads, writes)
        s = "c" + q
        cnt[s] = cnt.get(s, 0) + 1
        fn().then_inc(T.sem[s], 1)
        snap[(s, cnt[s])] = dict(know[q])
        after((s, cnt[s]), reads, writes)

    def dmas(q, s, moves, reads, writes):
        reads, writes = reads.split(), writes.split()
        before(q, reads, writes)
        for o, i in moves:
            Q[q].dma_start(o, i).then_inc(T.sem[s], 16)
        cnt[s] = cnt.get(s, 0) + 16 * len(moves)
        snap[(s, cnt[s])] = dict(know[q])
        after((s, cnt[s]), reads, writes)

    def arrives(s, n, tag):
        cnt[s] = n
        wr.setdefault(tag, []).append((s, n))

    def mm(calls, reads, writes):
        def run():
            last = None
            for a in calls:
                last = pe.matmul(*a)
            return last
        op("p", run, reads, writes)

    def ts(out, in0, s1, s2, o0, o1, reads, writes):
        if o1 is None:
            op("v", lambda: vec.tensor_scalar(out, in0, s1, None, o0), reads, writes)
        else:
            op("v", lambda: vec.tensor_scalar(out, in0, s1, s2, o0, o1), reads, writes)

    def tt(out, a, b, o, reads, writes):
        op("v", lambda: vec.tensor_tensor(out, a, b, o), reads, writes)

    def cp(out, a, reads, writes):
        op("v", lambda: vec.tensor_copy(out, a), reads, writes)

    def ms(out, val, writes):
        op("v", lambda: vec.memset(out, val), "", writes)

    def ac(out, a, f, bias, scale, reads, writes):
        op("a", lambda: act.activation(out, a, f, bias=bias, scale=scale), reads, writes)

    def io(out, pat, base, mul, writes, whole=False):
        if whole:
            op("g", lambda: g.iota(out, pat, base, mul), "", writes)
        else:
            op("g", lambda: g.iota(out, pat, base, mul, allow_small_or_imprecise_dtypes=True), "", writes)

    def weave(*seqs):
        seqs = [list(s) for s in seqs]
        while any(seqs):
            for s in seqs:
                if s:
                    s.pop(0)()

    ways = routes(T, topo, c)
    sent = [0]

    def send(ws, kind, src, there, on_way, sems, reads):
        trs = []
        for w in ws:
            k, dst, sem = (T.cores[w["d"]], there(w), sems[0]) if w["via"] is None else (w["via"], on_way, sems[1])
            rid, pid = topo.addr(k, core)
            sent[0] += len(w[kind])
            trs.append(RemoteDMATransfer(dst_ids=[DstId(rid=rid, pnc=pid)], dma_engine_mask=bits(w[kind]), remote_sem=T.sem[sem], src=src(w), dst=dst))
        before("g", reads.split(), [])
        g.remote_dma_fused(trs, local_sem=T.sem.sent)

    def coming(kind, h=0, near=(True, False)):
        who, n = [], 0
        for d in range(len(T.cores)):
            if d != c:
                for w in routes(T, topo, d):
                    if w["d"] == c and w["h"] == h and w["near"] in near and w[kind]:
                        who.append(d)
                        n += len(w[kind]) if w["via"] is None else len(topo.engines(w["via"], core))
        return who, n

    def xload(h, d, at):
        return (T.xi[:, at:at + 256], T.x[32 * d:32 * d + 32, 1024 * h:1024 * h + 1024])
    dmas("s", "lw", [(T.st[:, 0:4, :], T.w1[:]), (T.st[:, 4:8, :], T.w2[:])], "", "su")
    dmas("s", "lx0", [xload(0, w["d"], 256 * k) for k, w in enumerate(ways[0:2])], "", "xi0")
    dmas("a", "lsm", [(T.st[:, 8:72, :], T.pa[:]), (T.st[:, 72:136, :], T.pb[:])], "", "st")
    dmas("a", "lx2", [xload(1, w["d"], 768 + 256 * k) for k, w in enumerate(ways[3:5])], "", "xi2")
    dmas("s", "lx1", [xload(0, ways[2]["d"], 512)], "", "xi1")
    dmas("s", "lx3", [xload(1, ways[5]["d"], 1280)], "", "xi3")

    ms(T.kb[:], BIG, "kb")
    io(T.pi[:], [[32, 4]], 0, 1, "pi", True)
    io(T.jj[:], [[1, 144]], -15, 0, "jj")
    io(T.jg[:], [[16, 8], [0, 16]], 0, 0, "jg")
    send(ways, "small", lambda w: T.st[w["d"], 8 * w["h"]:8 * w["h"] + 128, :], lambda w: T.ds[c], T.rs[:], ("as0", "rsm"), "su st")
    dmas("s", "ow", [(T.ds[c, 0:72, :], T.st[c, 0:72, :])], "su st", "ds0")
    dmas("s", "osm", [(T.ds[4 + c, 64:128, :], T.st[c, 72:136, :])], "st", "ds1")
    FILL = 9
    for k in range(FILL):
        op("a", lambda: act.activation(T.tab[:, 1024 * k:1024 * k + 1024], T.kb[:], F.Silu), "kb", "tab%d" % k)
    ms(T.tab[:, 1024 * FILL:1024 * FILL + 1024], BIG, "tab%d" % FILL)

    def big(ks, reads):
        send([ways[k] for k in ks], "big", lambda w: T.xb[:, 256 * ways.index(w):256 * ways.index(w) + 256], lambda w: T.db[4 * w["h"] + c], T.rb[:],
             ("an0", "rbig"), reads)

    p = T.pi[:, 0:1]
    ts(T.ci[:, 0:4], T.pi[:], 112, None, A.bitwise_and, None, "pi", "ci0")
    ts(T.ci[:, 4:5], p, 15, None, A.bitwise_and, None, "pi", "ci1")
    ts(T.ci[:, 5:6], p, 31, None, A.bitwise_and, None, "pi", "ci2")
    ts(T.ci[:, 6:7], p, 3, 1, A.logical_shift_right, A.bitwise_and, "pi", "ci3")
    ts(T.ci[:, 7:8], p, 1, 7, A.logical_shift_right, A.bitwise_and, "pi", "ci4")
    ts(T.ci[:, 8:9], p, 1, None, A.bitwise_and, None, "pi", "ci5")
    ts(T.ci[:, 9:10], p, 4, 1, A.logical_shift_right, A.bitwise_and, "pi", "ci6")
    ts(T.ci[:, 10:11], p, 5, None, A.logical_shift_right, None, "pi", "ci7")
    ts(T.ci[:, 12:16], T.pi[:], 127, None, A.bitwise_and, None, "pi", "ci8")
    cp(T.xb[:, 0:512], T.xi[:, 0:512], "xi0", "xb0")
    big((0, 1), "xb0")
    cp(T.cf[:, 0:11], T.ci[:, 0:11], "ci0 ci1 ci2 ci3 ci4 ci5 ci6 ci7", "cf")
    cp(T.cf[:, 20:24], T.ci[:, 12:16], "ci8", "cfr")
    cp(T.xb[:, 768:1280], T.xi[:, 768:1280], "xi2", "xb2")
    big((3, 4), "xb2")
    dmas("s", "lx4", [xload(0, c, 1536)], "xb2", "xi4")
    dmas("s", "lx5", [xload(1, c, 1792)], "", "xi5")
    cp(T.xb[:, 512:768], T.xi[:, 512:768], "xi1", "xb1")
    cp(T.xb[:, 1280:1536], T.xi[:, 1280:1536], "xi3", "xb3")
    big((2, 5), "xb1 xb3")

    def lay_in(h, sem, who, tag):
        dmas("s", sem, [(T.xn[32 * r:32 * r + 32, 1024 * h:1024 * h + 1024], T.db[4 * h + r] if r != c else T.xb[:, 1536 + 256 * h:1792 + 256 * h])
                        for r in who], tag, "x" + tag)
    io(T.j32[:], [[0, 4], [1, 32]], 0, 0, "j32")
    io(T.jy[:], [[0, 4], [1, 2], [0, 16]], 0, 0, "jy")
    io(T.io8[:], [[16, 8]], 0, 0, "io8")
    io(T.tab[:, TW - V:TW], [[0, V]], int(BIG), 0, "tab%d tab%d" % (FILL + 1, FILL + 2))

    def col(k):
        return T.cf[:, k:k + 1]
    G0, G2, G6, C16, P31, HH, I2, ODD, YY, RK, PN, P2, P6 = [col(k) for k in (0, 1, 3, 4, 5, 6, 7, 8, 9, 10, 20, 21, 23)]
    J0 = T.jj[:, 15:143]
    ts(T.shn[:], J0, P6, None, A.is_equal, None, "cfr jj", "shn")
    ts(T.nshp[:], J0, P2, -1.0, A.is_equal, A.mult, "cfr jj", "nshp")
    ts(T.idb[:], J0, PN, None, A.is_equal, None, "cfr jj", "idb")
    ts(col(12), HH, 8.0, G6, A.mult, A.add, "cf", "c12")
    ts(col(13), HH, 4.0, G2, A.mult, A.add, "cf", "c13")
    ts(col(14), I2, G0, None, A.add, None, "cf", "c14")
    ts(col(15), ODD, 511.0, 1.0, A.mult, A.add, "cf", "c15")
    ts(col(16), C16, 128.0, float(TW), A.mult, A.add, "cf", "c16")
    ts(col(17), RK, -1.0, 3.0, A.mult, A.add, "cf", "c17")
    ts(col(19), I2, G2, None, A.add, None, "cf", "c19")
    ts(col(11), YY, 32.0, C16, A.mult, A.add, "cf", "c11")
    ts(T.k2[:], T.jj[:, 7:143], col(19), col(15), A.is_equal, A.mult, "c19 c15 jj", "k2")
    ts(T.idf[:], J0, PN, None, A.is_equal, None, "cfr jj", "idf")
    ts(T.nid[:], J0, PN, -4096.0, A.is_equal, A.mult, "cfr jj", "nid")
    ms(T.msk[:, 8:16], 0.0, "msk2")
    ms(T.crow[0:1, 0:4], -2047.5, "crow0")
    ms(T.crow[0:1, 4:7], 0.0, "crow1")
    ms(T.crow[0:1, 7:8], 2047.5, "crow2")
    ts(T.msk[:, 0:4], T.jj[:, 15:19], RK, None, A.is_equal, None, "cf jj", "msk0")
    ts(T.mtmp[:, 0:5], T.jj[:, 15:20], col(17), None, A.is_equal, None, "c17 jj", "mtmp")
    ms(T.ks[:], 0, "ks")
    ms(T.onef[0:1, :], 1.0, "onef")
    tt(T.msk[:, 4:8], T.mtmp[:, 0:4], T.mtmp[:, 1:5], A.subtract, "mtmp", "msk1")
    ms(T.kr[0:2, :], 1024.0, "kr")
    for h in range(2):
        cp(T.xb[:, 1536 + 256 * h:1792 + 256 * h], T.xi[:, 1536 + 256 * h:1792 + 256 * h], "xi%d" % (4 + h), "xo%d" % h)
        lay_in(h, "ob%d" % h, [c], "xo%d" % h)
    ts(T.zf[:], T.jj[:], G6, None, A.is_equal, None, "cf jj", "zf")
    ts(T.yf[:], T.jj[:], col(12), None, A.is_equal, None, "c12 jj", "yf")
    ts(T.kk[:], T.jj[:, 7:143], col(14), col(15), A.is_equal, A.mult, "c14 c15 jj", "kk")
    ts(T.e16[:], T.jj[:, 15:31], C16, 1.0e9, A.not_equal, A.mult, "cf jj", "e16")
    ts(T.nk2[:], T.k2[:], -1.0, None, A.mult, None, "k2", "nk2")
    ts(T.rr[:], T.j32[:], P31, None, A.is_equal, None, "cf j32", "rr")
    ts(T.e16[:], T.e16[:], float(TW), None, A.add, None, "e16", "e16")
    io(T.kr[0:1, :], [[1, 256]], 0, 0, "kr")
    io(T.jw[:], [[1, 164]], -33, 0, "jw")
    io(T.tab[:, TW:TD], [[0, V]], int(BIG), 0, "tabd")
    for h in range(2):
        arrives("as%d" % h, coming("small", h)[1], "ds%d" % h)
        arrives("an%d" % h, coming("big", h, (True,))[1], "dn%d" % h)
        arrives("af%d" % h, coming("big", h, (False,))[1], "df%d" % h)

    dmas("s", "gw", [(T.wi[:, 4 * u:4 * u + 1], T.ds[0:4, 4 * u:4 * u + 4, :]) for u in range(2)], "ds0", "wi")
    dmas("s", "gsm", [(T.sm[0:96, 16:32], T.ds[1:4, 8:72, :]), (T.sm[96:128, 16:32], T.ds[0, 8:72, :]), (T.sm[:, 0:16], T.ds[4:8, 64:128, :])], "ds0 ds1", "sm")
    lay_in(0, "gx0", coming("big", 0, (False,))[0], "df0")
    lay_in(0, "gy0", coming("big", 0, (True,))[0], "dn0")
    lay_in(1, "gx1", coming("big", 1, (False,))[0], "df1")
    lay_in(1, "gy1", coming("big", 1, (True,))[0], "dn1")
    XH = ["xxo0 xdn0 xdf0", "xxo1 xdn1 xdf1"]
    XA = XH[0] + " " + XH[1]
    dmas("s", "gp", [(T.pn[32:128, :], T.xn[0:96, :]), (T.pn[0:32, :], T.xn[96:128, :])], XA, "pn")
    dmas("s", "gs", [(T.sn[0:96, :], T.xn[32:128, :]), (T.sn[96:128, :], T.xn[0:32, :])], XA, "sn")

    ts(T.sg[:], T.jy[:], YY, 4.0, A.is_equal, A.mult, "cf jy", "sg")
    ms(T.mone[:], -1.0, "mone")
    ts(T.off[:], J0, col(16), None, A.add, None, "c16 jj", "off0 off1")
    ms(T.dw[:, 0:3], 128.0, "dw0")
    ms(T.dw[:, 3:4], 0.0, "dw1")
    ts(T.io8[:], T.io8[:], C16, None, A.add, None, "cf io8", "io8")
    ms(T.zer[:], 0.0, "zer")
    ms(T.dall[:, 256:272], NOD, "dall1")
    ms(T.oneb[0:2, :], 1.0, "oneb")
    ts(col(11), col(11), 2.0, None, A.mult, None, "c11", "c11")
    ts(T.nkk[:], T.kk[:], -1.0, None, A.mult, None, "kk", "nkk")
    ts(T.zr[:], T.jj[:], G2, 16384.0, A.is_equal, A.mult, "cf jj", "zr")
    ts(T.yr[:], T.jj[:], col(13), 16384.0, A.is_equal, A.mult, "c13 jj", "yr")
    ts(T.bg[:], T.jg[:], G0, -512.0, A.is_equal, A.mult, "cf jg", "bg")
    ts(T.bgs[:], T.jg[:], G2, -512.0, A.is_equal, A.mult, "cf jg", "bgs")
    cp(T.wf[:, 0:2], T.wi[:, 0:5:4], "wi", "wf")
    cp(T.wfb[:], T.wi[:, 0:5:4], "wi", "wfb")
    ZW, ZN, ZP = (T.zw0, T.zw1), (T.zn0, T.zn1), (T.zp0, T.zp1)
    mm([(T.ka[:, 0:2], T.shn[:], T.wfb[:], True, True), (T.ka[:, 2:4], T.nshp[:], T.wfb[:], True, True)], "shn nshp wfb", "pska")
    for u in range(2):
        ts(ZW[u][:], T.jj[:], G0, T.wf[:, u:u + 1], A.is_equal, A.mult, "cf jj wf", "zw%d" % u)
    cp(T.wf[:, 4:8], T.ka[:, 0:4], "pska", "wfs")
    ts(T.li[:, 32:64], T.sm[:], 6, 15, A.logical_shift_right, A.bitwise_and, "sm", "li1")
    ts(T.bw[:, 0:128], T.jg[:], G0, T.wf[:, 0:1], A.is_equal, A.mult, "cf jg wf", "bw0")
    cp(T.l7[:, 32:64], T.li[:, 32:64], "li1", "l7b")
    ac(T.thr[:], T.e16[:, 0:16].indirect(T.l7[:, 32:64]), F.Identity, 0.0, 1.0, "e16 l7b", "thr")
    ts(T.bw[:, 128:256], T.jg[:], G0, T.wf[:, 1:2], A.is_equal, A.mult, "cf jg wf", "bw1")
    mm([(T.ka[:, 0:256], T.rr[:], T.bw[:], True, True)], "rr bw0 bw1", "pska")
    for u in range(2):
        ts(ZN[u][:], T.jj[:], G2, T.wf[:, 4 + u:5 + u], A.is_equal, A.mult, "cf jj wfs", "zn%d" % u)
    cp(T.wm[:], T.ka[:, 0:256], "pska", "wm")
    cp(T.lp[:], T.sm[:], "sm", "lp")
    for u in range(2):
        ts(ZP[u][:], T.jj[:], G6, T.wf[:, 6 + u:7 + u], A.is_equal, A.mult, "cf jj wfs", "zp%d" % u)

    def later():
        return [lambda d=d: ts(T.wm4[:, 128 * d:128 * d + 128], T.wm[:, 128:256], T.msk[:, d:d + 1], None, A.mult, None, "wm msk0", "wm4%d" % d)
                for d in range(4)]

    def latest():
        ts(T.li[:, 0:32], T.sm[:], 63, None, A.bitwise_and, None, "sm", "li0")
        ts(T.li[:, 64:96], T.sm[:], 4, 64, A.logical_shift_right, A.bitwise_and, "sm", "li2")
        tt(T.li[:, 0:32], T.li[:, 0:32], T.li[:, 64:96], A.add, "li0 li2", "li0")
        cp(T.l7[:, 0:32], T.li[:, 0:32], "li0", "l7")

    def result_rows(r):
        ts(T.rl[:, 164 * r:164 * r + 164], T.jw[:], col(11), T.mtmp[:, 3 - r:4 - r], A.is_equal, A.mult, "c11 jw mtmp", "rl%d" % r)

    def places(k, a, n, u2, held, last, tags, out_tag):
        u1, m = T.hs[:, a:a + n], T.hm[:, a:a + n]
        hs, hm = "hs_%d" % k, "hm_%d" % k
        return [lambda: ts(u1, u1, 4095, None, A.bitwise_and, None, tags, hs),
                lambda: tt(m, u1, u2, A.mult, hs + " " + held, hm),
                lambda: ts(m, m, 5, 8191, A.logical_shift_right, A.bitwise_and, hm, hm),
                lambda: tt(m, m, u2, A.add, hm + " " + held, hm),
                lambda: cp(last, m, hm, out_tag)]

    MB = (T.m0, T.m1, T.m2, T.m3)
    ST = (T.st0, T.st1)
    PK = [((T.st0, "psst0"), (T.st1, "psst1"), (T.pq, "pspq"))[b] for b in PLAN["bank"]]

    def pack(bank, src, at, w, kk=T.kk, first=True, last=True, gap=0):
        b = at + (gap or w)
        return [(bank[:, 0:w], kk[:, 8:136], src[:, at:at + w], first, False), (bank[:, 0:w], kk[:, 0:128], src[:, b:b + w], False, last)]
    alone = [int(k[1:]) for k in PLAN["aq"].split() if k[0] == "e"]

    def scatter(h, src, reads, more=""):
        op("a", lambda: act.activation(T.tab[:, 0:TD if more else TW].indirect(T.kl[:, 64 * h:64 * h + 64]), src, F.Silu),
           "kl%d " % h + reads, "tab " + more)

    def own_sums(h, u):
        a = 1024 * h
        mm([(MB[h][:, 64 * u:64 * u + 64], ZW[u][:, 15 - k:143 - k], T.xn[:, a + 64 * k:a + 64 * k + 64], k == 0, k == 15) for k in range(16)],
           "zw%d %s" % (u, XH[h]), "psm%d" % h)

    def pred_sums(h, u):
        a = 1024 * h
        mm([(MB[2 + u][:, 0:64], ZN[u][:, 15 - k:143 - k], T.xn[:, a + k:a + 1024:16], k == 0, k == 15) for k in range(16)],
           "zn%d %s" % (u, XH[h]), "psm%d" % (2 + u))

    def pred_keep(h, u):
        ts(T.up[:, 128 * u + 64 * h:128 * u + 64 * h + 64], MB[2 + u][:, 0:64], LIFT * u, None, A.add, None, "psm%d" % (2 + u), "up%d_%d" % (u, h))

    def pred_pack(h):
        mm(pack((T.pq, T.m1)[h], T.xn, 1024 * h, 512, T.k2), "k2 " + XH[h], ("pspq", "psm1")[h])

    def pred_packed(h, a=0, b=512):
        o, tag = T.pc[:, 512 * h + a:512 * h + b], "pc%d" % h
        if h == 0:
            ac(o, T.pq[:], F.Identity, 64.0 * 513, 1.0, "pspq", tag)
        else:
            ts(o, T.m1[:, a:b], 64.0 * 513, None, A.add, None, "psm1", tag)

    def lay(h, k):
        a = 1024 * h
        o, i = T.xf[:, a + k:a + 1024:16], T.xn[:, a + 64 * k:a + 64 * k + 64]
        if h == 1:
            ts(o, i, 128.0, None, A.add, None, XH[h], "xf%d_%d" % (h, k))
        else:
            ac(o, i, F.Identity, 128.0, 1.0, XH[h], "xf%d_%d" % (h, k))

    def own_places(h):
        u12, u1, u2, m = T.ph[:, 0:128], T.ph[:, 0:64], T.ph[:, 64:128], T.ph[:, 128:192]
        return [lambda: cp(u12, MB[h][:, 0:128], "psm%d" % h, "ph"),
                lambda: ts(u12, u12, 4095, None, A.bitwise_and, None, "ph", "ph"),
                lambda: tt(m, u1, u2, A.mult, "ph", "pm"),
                lambda: ts(m, m, 5, 8191, A.logical_shift_right, A.bitwise_and, "pm", "pm"),
                lambda: tt(T.pos[:, 64 * h:64 * h + 64], m, u2, A.add, "ph pm", "pos%d" % h),
                lambda: cp(T.kl[:, 64 * h:64 * h + 64], T.pos[:, 64 * h:64 * h + 64], "pos%d" % h, "kl%d" % h)]

    def build(h):
        op("a", lambda: act.activation(T.tab[:, 0:TW].indirect(T.kl[:, 64 * h:64 * h + 64]), T.xf[:, 1024 * h:1024 * h + 1024], F.Silu),
           "kl%d " % h + " ".join("xf%d_%d" % (h, k) for k in range(16)), "tab " + " ".join("tab%d" % k for k in range(TW // 1024)))

    def differences(a, b, bank, tag):
        n = 16 * (b - a)
        mm([(bank[:, 0:n], T.idb[:], T.dtmp[:, 0:n], True, False), (bank[:, 0:n], T.nshp[:], T.dtmp[:, 256:256 + n], False, True)],
           "idb nshp dt0 dt1", tag)

    def u2_start(hs):
        for k in range(2):
            mm([(ST[k][:, 128 * d + 64 * hs[0]:128 * d + 64 * hs[-1] + 64], T.idf[:], T.up[:, 128 + 64 * hs[0]:192 + 64 * hs[-1]], d == 0 and hs[0] == 0, False)
                for d in range(2)], "idf up1_0 up1_%d" % hs[-1], "psst%d" % k)

    for u in range(2):
        own_sums(0, u)
    pred_pack(0)
    for k in range(16):
        lay(0, k)
    pred_packed(0)
    for u in (1, 0):
        pred_sums(0, u)
    weave(own_places(0), later() + [lambda: pred_keep(0, 1)])
    build(0)
    pred_keep(0, 0)
    u2_start((0,))
    own_sums(1, 0)
    for k in range(2):
        cp(T.dtmp[:, 256 * k:256 * k + 32], T.xn[:, 0:V].indirect(T.lp[:, 16 * k:16 * k + 2]), XA + " lp", "dt%d" % k)
    differences(0, 2, T.ka, "pska")
    own_sums(1, 1)
    steps = own_places(1)
    fillers = [lambda k=k: lay(1, k) for k in range(6)]
    for k in range(5):
        fillers += [steps[k], lambda k=k: lay(1, 6 + 2 * k), lambda k=k: lay(1, 7 + 2 * k)]
    fillers += steps[5:]

    def fill(n):
        for f in fillers[:n]:
            f()
        del fillers[:n]
    fill(4)
    cp(T.dall[:, 0:32], T.ka[:, 0:32], "pska", "dall0")
    pred_sums(1, 1)
    fill(2)

    tabw = T.tab[:, 0:TW]

    def winner_out(t, a=0, b=6):
        y, w128, m = T.yt[:, 4 * t:4 * t + 4], T.sw[:, 4 * t + 3:4 * t + 4], T.mk[:, t:t + 1]
        for args in [(y[:, 0:1], w128, F.Identity, 0.25, 1.0 / 512, "sw%d" % t, "yt0"),
                     (y[:, 1:2], w128, F.Identity, 1.0, 1.0 / 128, "sw%d" % t, "yt1"),
                     (y[:, 2:3], m, F.Identity, y[:, 0:1], 0.25, "mk%d yt0" % t, "yt2"),
                     (y[:, 3:4], y[:, 2:3], F.Sign, -1.0, 1.0, "yt2", "yt3"),
                     (T.ryw[:, t:t + 1], y[:, 3:4], F.Identity, -1.0, y[:, 1:2], "yt3 yt1", "rw%d" % t),
                     (T.ryw[:, 4 + t:5 + t], y[:, 3:4], F.Identity, -1.0, y[:, 2:3], "yt3 yt2", "rc%d" % t)][a:b]:
            ac(*args)

    def results(t, js, tag):
        order = [w["d"] for w in ways[0:3]] + [c]
        mm([(T.m3[:, 32 * k:32 * k + 32], T.rl[:, 164 * r + 33 - s:164 * r + 161 - s], T.cov[:, 128 * t + 32 * j:128 * t + 32 * j + 32],
             t + j + k == 0, t == RO - 1 and j == 3 and k == 3)
            for j, s in enumerate((0, 1, 32, 33)) if j in js for k, r in enumerate(order)], "rl0 rl1 rl2 rl3 " + tag, "psm3")

    for t in range(RO):
        last = t == RO - 1
        dwin, dtag = (T.dall[:, 0:32], "dall0") if t == 0 else (T.dall[:, 0:272], "dall0 dall1 dall2")
        mm([(T.ka[:, 16:24], T.onef[0:1, :], T.crow[0:1, :], True, False)], "onef crow0 crow1 crow2", "pska")
        tt(T.dm[:], dwin.indirect(T.ks[:, 0:1]), T.msk[:], A.mult, dtag + " ks msk0 msk1 msk2", "dm")
        mm([(T.ka[:, 16:24], T.wm[:, 128:256], T.dm[:, 0:8], False, True), (T.ka[:, 8:16], T.wm[:, 0:128], T.dm[:, 0:8], True, True),
            (T.ka[:, 0:8], T.rr[:], T.dm[:, 0:8], True, True)], "wm rr dm", "pska")
        cp(T.dbc[:], dwin.indirect(T.ks[:]), dtag + " ks", "dbc")
        if t == 0:
            fill(4)
            pred_keep(1, 1)
            pred_sums(1, 0)
            fill(len(fillers))
            build(1)
            u2_start((1,))
        for k in range(2):
            mm([(ST[k][:, 128 * d:128 * d + 128], T.wm4[:, 256 * k + 128 * d:256 * k + 128 * d + 128], T.dbc[:], False, False) for d in range(2)],
               "wm4%d wm4%d dbc" % (2 * k, 2 * k + 1), "psst%d" % k)
        if t == 0:
            pred_keep(1, 0)

        def quotients(k):
            def one(d):
                ts(T.kq[:, 128 * d:128 * d + 128], T.up[:, 128:256], T.ka[:, 16 + d:17 + d], 1.0 / 4096, A.add, A.mult, "up1_0 up1_1 pska", "kq%d" % d)
                if d % 2:
                    mm([(ST[k][:, 0:256], T.nid[:], T.kq[:, 256 * k:256 * k + 256], False, True)], "nid kq%d kq%d" % (d - 1, d), "psst%d" % k)
            return [lambda d=d: one(d) for d in (2 * k, 2 * k + 1)]

        def sums(k):
            return [lambda d=d: ts(T.hs[:, 128 * d:128 * d + 128], T.up[:, 0:128], T.ka[:, 8 + d:9 + d], None, A.add, None,
                                   "up0_0 up0_1 pska hs_%d" % k, "hs%d" % d) for d in (2 * k, 2 * k + 1)]
        weave(quotients(0) + sums(0))
        cp(T.av[:], T.ka[:, 0:24], "pska", "av")
        first = places(0, 0, 256, ST[0][:, 0:256], "psst0", T.lf[:, 0:256], "hs0 hs1", "lf0")
        second = places(1, 256, 256, ST[1][:, 0:256], "psst1", T.lf[:, 256:512], "hs2 hs3", "lf1")
        weave(first[0:1] + sums(1) + first[1:2] + quotients(1))
        if t == 0:
            pred_pack(1)
            for u in range(2):
                mm([(T.pq[:, 128 * u:128 * u + 128], ZP[u][:, 15 - k:143 - k], T.xn[:, k::16], k == 0, k == 15) for k in range(16)], "zp%d %s" % (u, XA), "pspq")
        else:
            for d in range(4):
                mm([(MB[d][:, 0:128], T.nid[:], T.cov[:, 128 * t - 128:128 * t], True, False)], "nid cov%d" % (t - 1), "psm%d" % d)
        mm([(T.ka[:, 32:36], T.onef[0:1, :], T.jj[0:1, 15:19], True, False)], "onef jj", "pska")
        weave(first[2:4], second[0:2])
        ts(T.ba[:], T.av[:, 0:4], -1.0, -64.0, A.mult, A.add, "av", "ba")
        weave(first[4:5] + second[2:3])
        ts(T.cd[:], T.av[:, 0:4], 128.0, None, A.add, None, "av", "cd")
        weave([lambda k=k: pred_packed(1, 256 * k, 256 * k + 256) for k in range(2)] if t == 0 else
              [lambda: result_rows(t), lambda: result_rows(0) if t == 1 else
               tt(T.cov[:, 0:128], T.cov[:, 0:128], T.cov[:, 128 * t - 128:128 * t], A.add, "cov0 cov%d" % (t - 1), "cov0")], second[3:5])

        begun = [t > 0] * 4
        left = [V] * 4

        def lst(d, a, n):
            return T.lf[:, 128 * d + a // 16:128 * d + (a + n) // 16]

        def blocks(bank, z, src, at, a, n, first, last):
            h, k = a // 1024, a % 1024 // 64
            return [(bank[:, 64 * h:64 * h + 64], z[:, 15 - k - b:143 - k - b], src[:, at + 64 * b:at + 64 * b + 64], first and b == 0, last and b == n - 1)
                    for b in range(n)]

        def into(d, z, src, at, a, n, notes, tags):
            left[d] -= notes
            mm(blocks(MB[d], z, src, at, a, n, not begun[d], left[d] == 0), tags, "psm%d" % d)
            begun[d] = True

        def a_get(k, d, a, w):
            at = 1024 * (k % 3)
            for j, (b, n) in enumerate([(a, 1024)] if w == 512 else [(a, w), (a + 512, w)]):
                ac(T.ab[:, at + w * j:at + w * j + n], tabw.indirect(lst(d, b, n)), F.Identity, T.ba[:, d:d + 1], 1.0,
                   "tab ba lf%d" % (d // 2), "ab%d ac%d" % (k % 3, k % 3) if n == 1024 else "a%s%d" % ("bc"[j], k % 3))

        def a_pre(k, d, a, w):
            mm(pack(PK[k][0], T.xn, a, w, T.nk2, True, False, 512), "nk2 " + XA, PK[k][1])

        def a_pack(k, d, a, w):
            mm(pack(PK[k][0], T.ab, 1024 * (k % 3), w, T.kk, k not in alone), "kk ab%d ac%d" % (k % 3, k % 3), PK[k][1])

        def a_test(k, d, a, w):
            ac(T.fc[:, 512 * (k % 3):512 * (k % 3) + w], PK[k][0][:, 0:w], F.Abs, -64.0 * 513, 1.0, PK[k][1], "fc%d" % (k % 3))

        def a_cmp(k, d, a, w):
            at = a // 1024 * 512 + a % 1024
            tt(T.fc[:, 512 * (k % 3):512 * (k % 3) + w], PK[k][0][:, 0:w], T.pc[:, at:at + w], A.not_equal,
               "%s pc%d" % (PK[k][1], a // 1024), "fc%d" % (k % 3))

        def a_sum(k, d, a, w):
            into(d, T.yf, T.fc, 512 * (k % 3), a, w // 64, 2 * w, "yf fc%d" % (k % 3))

        def v_get(k, d, a, n):
            tt(T.eb[:, 1024 * (k % 3):1024 * (k % 3) + n], tabw.indirect(lst(d, a, n)), T.pn[:, a:a + n], A.subtract,
               "tab pn lf%d" % (d // 2), "eb%d" % (k % 3))

        def v_cmp(k, d, a, n):
            e = T.eb[:, 1024 * (k % 3):1024 * (k % 3) + n]
            ts(e, e, T.cd[:, d:d + 1], None, A.not_equal, None, "cd eb%d" % (k % 3), "eb%d" % (k % 3))

        def v_sum(k, d, a, n):
            into(d, T.zf, T.eb, 1024 * (k % 3), a, n // 64, n, "zf eb%d" % (k % 3))

        def count(d):
            op("a", lambda: act.activation(T.fit[:, 128 * d:128 * d + 128], MB[d][:, 0:128], F.Relu, bias=1.0, scale=-1.0,
                                           accum_out=T.cn[:, 3 - d:4 - d]), "psm%d" % d, "fit%d cn%d" % (d, d))

        jobs = {}
        for j, u in enumerate(PLAN["a"]):
            test, w = "t%d" % j, u[2]
            prev = ["t%d" % i for i in range(j) if PLAN["bank"][i] == PLAN["bank"][j]]
            jobs["ag%d" % j] = ("a", ["pk%d" % (j - 3)], 2.7 * w + 60, a_get, (j,) + u)
            if j in alone:
                jobs["pr%d" % j] = ("p", prev + ["ag%d" % (j - 1)], 0.9 * w, a_pre, (j,) + u)
            jobs["pk%d" % j] = ("p", prev + ["ag%d" % j, "pr%d" % j], 0.9 * w, a_pack, (j,) + u)
            jobs[test] = ("a" if j in alone else "v", ["pk%d" % j, "as%d" % (j - 3)], 0.9 * w, a_test if j in alone else a_cmp, (j,) + u)
            jobs["as%d" % j] = ("p", [test], 0.45 * w, a_sum, (j,) + u)
        for k, u in enumerate(PLAN["v"]):
            jobs["vg%d" % k] = ("v", ["vs%d" % (k - 3)], 1.35 * u[2] + 50, v_get, (k,) + u)
            jobs["vc%d" % k] = ("v", ["vg%d" % k], 0.45 * u[2], v_cmp, (k,) + u)
            jobs["vs%d" % k] = ("p", ["vc%d" % k], 0.45 * u[2], v_sum, (k,) + u)
        for d in range(4):
            jobs["n%d" % d] = ("a", ["as%d" % j for j, u in enumerate(PLAN["a"]) if u[0] == d] + ["vs%d" % k for k, u in enumerate(PLAN["v"]) if u[0] == d],
                               130, count, (d,))
        line = {"a": [{"g": "ag", "e": "t", "n": "n"}[k[0]] + k[1:] for k in PLAN["aq"].split()],
                "v": [{"g": "vg", "c": "vc", "p": "t"}[k[0]] + k[1:] for k in PLAN["vq"].split()]}
        free, done = {"a": 0.0, "v": PLAN["lag"], "p": 0.0}, {}
        while len(done) < len(jobs):
            can = [k for k in line["a"][:1] + line["v"][:1] + [k for k in jobs if jobs[k][0] == "p" and k not in done]
                   if all(x in done for x in jobs[k][1] if x in jobs)]
            when = {k: max([free[jobs[k][0]]] + [done[x] + 100 for x in jobs[k][1] if x in jobs]) for k in can}
            k = min(can, key=lambda k: (when[k] - (PLAN["ahead"] if k[:2] == "pk" else 0), k))
            at = when[k]
            q, _, ns, fn, args = jobs[k]
            fn(*args)
            free[q] = done[k] = at + ns
            if q != "p":
                line[q].pop(0)
            if t == 0 and k == "ag1":
                for u in range(2):
                    ac(T.us[:, 128 * u:128 * u + 128], T.pq[:, 128 * u:128 * u + 128], F.Identity, LIFT * u, -1.0, "pspq", "us%d" % u)

        if t == 0:
            latest()

        mm([(T.ka[:, 32:36], T.sg[:], T.cn[:], False, True)], "sg cn0 cn1 cn2 cn3", "pska")
        if t == 0:
            for k in range(2):
                ac(T.dtmp[:, 256 * k:256 * k + 224], T.xn[:, 0:V].indirect(T.lp[:, 16 * k + 2:16 * k + 16]), F.Identity, 0.0, 1.0, XA + " lp", "dt%d" % k)
        else:
            winner_out(t - 1)
        mm([(T.pq[:, 0:128], T.idf[:], T.us[:, 128:256], True, False)], "idf us1", "pspq")
        if t == RO - 1:
            results(0, (0, 1, 2, 3), "cov0")
        m = T.mk[:, t:t + 1]
        op("v", lambda: vec.tensor_reduce(m, T.ka[:, 32:36], AxisListType.X, A.max), "pska", "mk%d" % t)
        ts(T.ns[:], T.ka[:, 32:36], m, None, A.not_equal, None, "pska mk%d" % t, "ns")

        def pick(out, src, tag):
            op("v", lambda: vec.tensor_tensor_scan(out, T.ns[:], src, 0.0, A.mult, A.add), "ns av dw0 dw1", tag)
        pick(T.sel[:, 8:12], T.av[:, 4:8], "sel2")
        pick(T.sel[:, 4:8], T.av[:, 20:24], "sel1")
        pick(T.sel[:, 0:4], T.av[:, 12:16], "sel0")
        W, w128 = T.sel[:, 11:12], T.sw[:, 4 * t + 3:4 * t + 4]
        ac(T.dbc[:], T.mone[:], F.Identity, 0.0, W, "mone sel2", "dbc")
        mm([(T.pq[:, 0:128], T.bw[:, 128:256], T.dbc[:], False, False)], "bw1 dbc", "pspq")
        pick(T.sw[:, 4 * t:4 * t + 4], T.dw[:], "sw%d" % t)
        ts(T.kq[:, 0:128], T.us[:, 128:256], T.sel[:, 7:8], 1.0 / 4096, A.subtract, A.mult, "us1 sel1", "kq0")
        mm([(T.pq[:, 0:128], T.nid[:], T.kq[:, 0:128], False, True)], "nid kq0", "pspq")
        for h in range(2):
            ts(T.hs[:, 64 * h:64 * h + 64], T.us[:, 64 * h:64 * h + 64], T.sel[:, 3:4], None, A.subtract, None, "us0 sel0 hs_0 hs_1 hs0", "hw%d" % h)
        weave(places(0, 0, 64, T.pq[:, 0:64], "pspq", T.lr[:, 0:64], "hw0", "lr0"),
              places(1, 64, 64, T.pq[:, 64:128], "pspq", T.lr[:, 64:128], "hw1", "lr1"),
              [lambda: ts(T.ofw[:], T.io8[:], w128, None, A.add, None, "io8 sw%d" % t, "ofw")])
        BK = (T.m0, T.m2)
        for h in range(2):
            mm(pack(ST[h], T.sn, 1024 * h, 256, T.nkk, True, False), "nkk sn", "psst%d" % h)
            if not last:
                mm([(BK[h][:, 64 * h:64 * h + 64], T.idf[:], T.pos[:, 64 * h:64 * h + 64], True, False)], "idf pos%d" % h, "psm%d" % (2 * h))
        mm([(T.m1[:, 0:128], T.idf[:], T.pos[:], True, False)], "idf pos0 pos1", "psm1")
        ac(T.br[:, 0:1], W, F.Identity, -64.0, 1.0, "sel2", "br")
        ac(T.cr[:, 0:1], W, F.Identity, 128.0, -1.0, "sel2", "cr")
        if last:
            winner_out(t, 0, 3)
        ac(T.nf[:], T.fit[:, 0:512].indirect(T.ofw[:]), F.Identity, 16384.0, -16384.0, "fit0 fit1 fit2 fit3 ofw", "nf")
        mm([(T.m1[:, 0:128], T.idb[:], T.nf[:], False, True)], "idb nf", "psm1")
        if last:
            winner_out(t, 3, 6)
            tags = " ".join("rw%d rc%d" % (k, k) for k in range(RO))
            dmas("s", "oy", [(T.dy[c], T.ryw[0:32, :])], tags, "dy")
            send(ways[0:3], "win", lambda w: T.dy[c], lambda w: T.dy[c], T.rw[:], ("ay", "rwin"), "dy")

        for h in range(2):
            ac(T.ab[:, 1024 * h:1024 * h + 512], tabw.indirect(T.lr[:, 64 * h:64 * h + 32]), F.Identity, T.br[:, 0:1], 1.0, "tab lr%d br" % h, "ab%d ac%d" % (h, h))
            mm(pack(ST[h], T.ab, 1024 * h, 256, T.kk, False, True), "kk ab%d" % h, "psst%d" % h)
            tt(T.eb[:, 1024 * h:1024 * h + 512], tabw.indirect(T.lr[:, 64 * h + 32:64 * h + 64]), T.sn[:, 1024 * h + 512:1024 * h + 1024], A.subtract,
               "tab lr%d sn" % h, "eb%d" % h)
            e = T.eb[:, 1024 * h:1024 * h + 512]
            if h == 0:
                tt(T.bb[:], T.m1[:, 0:128], T.off[:], A.min, "psm1 off0 off1", "bb")
            elif last:
                ts(T.cov[:, 128:256], T.bb[:], float(TW), -2.0 ** 60, A.is_lt, A.mult, "bb", "cov1")
            ts(e, e, T.cr[:, 0:1], None, A.not_equal, None, "cr eb%d" % h, "eb%d" % h)
            if h == 0:
                mm(blocks(BK[0], T.zr, T.eb, 0, 512, 8, last, False), "zr eb0", "psm0")
        for h in range(2):
            ac(T.fc[:, 512 * h:512 * h + 256], ST[h][:, 0:256], F.Abs, -64.0 * 513, 1.0, "psst%d" % h, "fc%d" % h)
            if h == 1:
                mm(blocks(BK[1], T.zr, T.eb, 1024, 1536, 8, last, False), "zr eb1", "psm2")
            if last:
                mm([(BK[h][:, 64 * h:64 * h + 64], T.idb[:], T.cov[:, 128 + 64 * h:192 + 64 * h], False, False)], "idb cov1", "psm%d" % (2 * h))
            mm(blocks(BK[h], T.yr, T.fc, 512 * h, 1024 * h, 4, False, True), "yr fc%d" % h, "psm%d" % (2 * h))
            if last:
                ts(T.cov[:, 384 + 64 * h:448 + 64 * h], BK[h][:, 64 * h:64 * h + 64], 0.5, float(RO), A.is_lt, A.mult, "psm%d" % (2 * h), "cov3_%d" % h)
            else:
                o = T.off[:, 64 * h:64 * h + 64]
                tt(o, BK[h][:, 64 * h:64 * h + 64], T.bb[:, 64 * h:64 * h + 64], A.min, "psm%d bb" % (2 * h), "off%d" % h)
                cp(T.kl[:, 64 * h:64 * h + 64], o, "off%d" % h, "kl%d" % h)
        if not last:
            for h in range(2):
                scatter(h, T.kb[:], "kb", "tabd")
            u2_start((0, 1))
            mm([(T.pq[:, 0:256], T.oneb[0:2, :], T.kr[0:2, :], True, False)], "oneb kr", "pspq")
            if t == 0:
                differences(2, 16, T.m3, "psm3")
            tt(T.pf[:], T.off[:, 0:128].indirect(T.l7[:, 0:32]), T.thr[:], A.is_ge, "off0 off1 l7 thr", "pf")
            mm([(T.pq[:, 0:256], T.bg[:], T.pf[:, 0:256], False, False), (T.pq[:, 0:256], T.bgs[:], T.pf[:, 256:512], False, True)],
               "bg bgs pf", "pspq")
            ts(T.cov[:, 128 * t:128 * t + 128], T.off[:], float(TW), -1.0, A.is_lt, A.mult, "off0 off1", "cov%d" % t)
            if t == 0:
                cp(T.dall[:, 32:256], T.m3[:, 0:224], "psm3", "dall2")
            op("v", lambda: vec.tensor_reduce(T.kmin[:, 0:1], T.pq[:, 0:256], AxisListType.X, A.min), "pspq", "kmin")
            ts(T.ks[:], T.zer[:], T.kmin[:, 0:1], float(PP), A.add, A.min, "kmin zer", "ks")

    for h in range(2):
        results(RO - 1, (2 * h, 2 * h + 1), "cov3_%d" % h)
    cp(T.res[:], T.m3[:, 0:128], "psm3", "res")
    for ws in (ways[0:2], ways[2:3]):
        send(ws, "last", lambda w: T.res[:, 32 * ways.index(w):32 * ways.index(w) + 32], lambda w: T.df[c], T.ro[:], ("al", "rlast"), "res")
    dmas("s", "of", [(T.df[c], T.res[:, 96:128])], "res", "df")
    arrives("ay", coming("win")[1], "dy")
    arrives("al", coming("last")[1], "df")
    dmas("a", "fiy", [(T.yw[y:8:2, :], T.dy[:, 64 * y:64 * y + 4, :]) for y in range(2)], "dy", "")
    dmas("s", "fin", [(T.yc[:], T.df[:])], "df", "")
    cnt["sent"] = sent[0]
    for s in cnt:
        if seen.get(s, 0) < cnt[s]:
            need("g", (s, cnt[s]))
